import numpy as np
import ml_dtypes


def mxq(x, axis, fmt="e4m3"):
    dtype, down = {"e4m3": (ml_dtypes.float8_e4m3fn, 7), "e5m2": (ml_dtypes.float8_e5m2, 14)}[fmt]
    v = np.moveaxis(np.asarray(x, np.float32).astype(ml_dtypes.bfloat16).astype(np.float64), axis, -1)
    blocks = v.reshape(v.shape[:-1] + (-1, 32))
    amax = np.abs(blocks).max(-1, keepdims=True)
    byte = np.maximum(np.where(amax > 0, np.frexp(amax)[1] - 1 + 127, 0) - down, 1)
    scale = np.exp2(byte - 127.0)
    codes = (blocks / scale).astype(np.float32).astype(dtype).astype(np.float64)
    return np.moveaxis((codes * scale).reshape(v.shape), -1, axis)


WIDE = False


def mx_kscale(k):
    if not WIDE:
        return np.ones(k)
    levels = np.array([10, -10, 5, -5, 0])
    if k % 512:
        return np.exp2(np.random.permutation(np.resize(levels, k // 32))).repeat(32)
    a = np.empty((k // 512, 16))
    for p in range(k // 512):
        a[p, :8] = np.random.permutation(np.resize(levels, 8))
        for g in range(8):
            far = levels[np.abs(levels - a[p, g]) >= 10]
            a[p, g + 8] = far[np.random.randint(len(far))]
    return np.exp2(a.ravel()).repeat(32)


def f64(x):
    return np.asarray(x).astype(np.float64)


def striped(idx):
    return np.tile(idx.reshape(-1, 16).T, (8, 1)).astype(np.uint16)


def unstriped(offs):
    return offs[:16].T.reshape(-1).astype(np.int64)


def relu(v):
    return np.maximum(v, 0.0)


K, T, D, S, V, H, N = 512, 512, 4, 1024, 256, 512, 256


def setup_inputs():
    n = np.random.standard_normal
    s = mx_kscale(K)[:, None]
    u = mx_kscale(H)
    return {
        "xT": (n((K, T)) * s).astype(np.float32),
        "w1": (n((K, H)) / np.sqrt(K) / s * u).astype(np.float32),
        "w2": (n((H, N)) / np.sqrt(H) / u[:, None]).astype(np.float32),
        "offs": striped(np.concatenate([np.random.permutation(T)[:V] for _ in range(D)])),
    }


def reference(xT, w1, w2, offs):
    idx = unstriped(offs)
    x = np.empty((K, V))
    for l in range(D):
        r = l // 4 * (4 * K // D) + l % 4 + 4 * np.arange(K // D)
        x[r] = f64(xT)[r][:, idx[l * V:(l + 1) * V]]
    xq = mxq(x, 0, "e4m3")
    h = relu(mxq(f64(w1), 0, "e4m3").T @ xq)
    return mxq(f64(w2), 0, "e4m3").T @ mxq(h, 0, "e4m3")

@@ -1,0 +1,165 @@
+from contextlib import ExitStack
+
+import concourse.mybir as mybir
+
+K, T, D, V, H, N = 512, 512, 4, 256, 512, 256
+P = 128
+FLOPS = 2 * K * H * V + 2 * H * N * V
+
+F32 = mybir.dt.float32
+BF16 = mybir.dt.bfloat16
+U32 = mybir.dt.uint32
+U16 = mybir.dt.uint16
+U8 = mybir.dt.uint8
+FP8X4 = mybir.dt.float8_e4m3fn_x4
+RELU = mybir.ActivationFunctionType.Relu
+
+CHUNKS = [(0, 128), (128, 256), (256, 384), (384, 512)]
+HALF = 128
+
+
+def tile_picked_grid_mlp_relu_sub_l_kernel(tc, xT, w1, w2, offs, out):
+    nc = tc.nc
+    with ExitStack() as ctx:
+        keep = ctx.enter_context(tc.tile_pool(name="keep", bufs=1))
+        psum = ctx.enter_context(tc.psum_pool(name="psum", bufs=1))
+
+        offsets = keep.tile([P, D * V // 16], U16, name="offsets")
+        nc.sync.dma_start(offsets[:], offs)
+        x_rows = xT.rearrange("(p l) w -> p l w", l=4)
+        tables = []
+        for l in range(4):
+            table = keep.tile([P, T], F32, name=f"table{l}")
+            nc.sync.dma_start(table[:], x_rows[:, l, :])
+            tables.append(table)
+        w1_rows = w1.rearrange("(p j) i -> p j i", j=4)
+        w1_raw = []
+        for c, (a, b) in enumerate(CHUNKS):
+            raw = keep.tile([P, 4, b - a], F32, name=f"w1_raw{c}")
+            nc.sync.dma_start(raw[:], w1_rows[:, :, a:b])
+            w1_raw.append(raw)
+        w2_rows = w2.rearrange("(c t q) n -> t c q n", t=4, q=4)
+        w2_raw = keep.tile([P, 4, N], F32, name="w2_raw", tag="w2_then_h", align_bytes=64)
+        for t in range(4):
+            nc.sync.dma_start(w2_raw[:, t, :], w2_rows[t])
+
+        x_picked = keep.tile([P, 4, V], F32, name="x_picked")
+        x_grouped = keep.tile([P, V, 4], BF16, name="x_grouped", align_bytes=64)
+        x_codes = keep.tile([P, V], U32, name="x_codes", align_bytes=64)
+        x_scales = keep.tile([P, V], U8, name="x_scales", align_bytes=64)
+        w1_grouped = keep.tile([P, 4, 128, 4], BF16, name="w1_grouped", align_bytes=64)
+        w1_codes = keep.tile([P, 4, 128], U32, name="w1_codes", align_bytes=64)
+        w1_scales = keep.tile([P, 4, 128], U8, name="w1_scales", align_bytes=64)
+        w2_grouped = keep.tile([P, N, 4], BF16, name="w2_grouped", align_bytes=64)
+        w2_codes = keep.tile([P, N], U32, name="w2_codes", align_bytes=64)
+        w2_scales = keep.tile([P, N], U8, name="w2_scales", align_bytes=64)
+
+        def w1_copy(copy, c, t0, t1):
+            a, b = CHUNKS[c]
+            dst = w1_grouped[:, t0:t1, a // 4 : b // 4, :].rearrange("p t (c q) j -> p t c j q", q=4)
+            src = w1_raw[c][:].rearrange("p j (c t q) -> p t c j q", t=4, q=4)[:, t0:t1]
+            copy(out=dst, in_=src)
+
+        cols = V // 16
+
+        def gather(l, v0, v1):
+            c0, c1 = l * cols + v0 // 16, l * cols + v1 // 16
+            nc.vector.tensor_copy(x_picked[:, l, v0:v1], tables[l][:].indirect(offsets[:, c0:c1]))
+
+        def x_copy(half):
+            v = slice(half * HALF, (half + 1) * HALF)
+            nc.vector.tensor_copy(
+                out=x_grouped[:, v, :].rearrange("p (c i) t -> p c t i", i=4),
+                in_=x_picked[:, :, v].rearrange("p t (c i) -> p c t i", i=4),
+            )
+
+        def quantize_x(half):
+            v = slice(half * HALF, (half + 1) * HALF)
+            nc.vector.quantize_mx(
+                out=x_codes[:, v].bitcast(FP8X4),
+                scales=x_scales[:, v],
+                in_=x_grouped[:, v, :].rearrange("p v t -> p (v t)"),
+            )
+
+        def quantize_w1(t):
+            nc.vector.quantize_mx(
+                out=w1_codes[:, t, :].bitcast(FP8X4),
+                scales=w1_scales[:, t, :],
+                in_=w1_grouped[:, t, :, :].rearrange("p m j -> p (m j)"),
+            )
+
+        def w2_copy(copy, u):
+            n = slice(u * 128, (u + 1) * 128)
+            copy(
+                out=w2_grouped[:, n, :].rearrange("p (c i) t -> p c t i", i=4),
+                in_=w2_raw[:, :, n].rearrange("p t (c i) -> p c t i", i=4),
+            )
+
+        hidden = [psum.tile([P, 4, HALF], F32, name=f"hidden{half}") for half in range(2)]
+
+        def mm1(t, half):
+            v = slice(half * HALF, (half + 1) * HALF)
+            nc.tensor.matmul_mx(
+                out=hidden[half][:, t, :],
+                lhsT=w1_codes[:, t, :].bitcast(FP8X4),
+                lhsT_scale=w1_scales[:, t, :],
+                rhs=x_codes[:, v].bitcast(FP8X4),
+                rhs_scale=x_scales[:, v],
+                start=True,
+                stop=True,
+            )
+
+        for l in range(3):
+            gather(l, 0, V)
+        for half in range(2):
+            gather(3, half * HALF, (half + 1) * HALF)
+        for c in range(3):
+            w1_copy(nc.scalar.copy, c, 0, 4)
+        for half in range(2):
+            x_copy(half)
+        for half in range(2):
+            quantize_x(half)
+        w1_copy(nc.scalar.copy, 3, 0, 2)
+        w1_copy(nc.scalar.copy, 3, 2, 4)
+        for t in range(4):
+            quantize_w1(t)
+            for half in range(2):
+                mm1(t, half)
+        w2_copy(nc.scalar.copy, 0)
+        w2_copy(nc.vector.tensor_copy, 1)
+        h_codes, h_scales = [], []
+        h_both = keep.tile([P, V, 4], BF16, name="h_both", tag="w2_then_h", align_bytes=64)
+        h_grouped = [h_both[:, half * HALF : (half + 1) * HALF, :] for half in range(2)]
+        for half in range(2):
+            h_codes.append(keep.tile([P, HALF], U32, name=f"h_codes{half}", align_bytes=64))
+            h_scales.append(keep.tile([P, HALF], U8, name=f"h_scales{half}", align_bytes=64))
+        nc.vector.quantize_mx(
+            out=w2_codes[:].bitcast(FP8X4), scales=w2_scales[:], in_=w2_grouped[:].rearrange("p n t -> p (n t)")
+        )
+        nc.scalar.activation(h_grouped[0], hidden[0][:].rearrange("p t v -> p v t"), RELU)
+        nc.vector.tensor_scalar_max(h_grouped[1], hidden[1][:].rearrange("p t v -> p v t"), 0.0)
+        out_view = out.rearrange("(u p) v -> p u v", u=2)
+        for half in range(2):
+            nc.vector.quantize_mx(
+                out=h_codes[half][:].bitcast(FP8X4),
+                scales=h_scales[half][:],
+                in_=h_grouped[half].rearrange("p v t -> p (v t)"),
+            )
+            acc = psum.tile([P, 2, HALF], F32, name=f"acc{half}")
+            for u in range(2):
+                n = slice(u * 128, (u + 1) * 128)
+                nc.tensor.matmul_mx(
+                    out=acc[:, u, :],
+                    lhsT=w2_codes[:, n].bitcast(FP8X4),
+                    lhsT_scale=w2_scales[:, n],
+                    rhs=h_codes[half][:].bitcast(FP8X4),
+                    rhs_scale=h_scales[half][:],
+                    start=True,
+                    stop=True,
+                )
+            result = keep.tile([P, 2, HALF], F32, name=f"result{half}")
+            if half == 0:
+                nc.scalar.copy(result[:], acc[:])
+            else:
+                nc.vector.tensor_copy(result[:], acc[:])
+            nc.sync.dma_start(out_view[:, :, half * HALF : (half + 1) * HALF], result[:])

@@ -13,9 +13,10 @@ U16 = mybir.dt.uint16
 U8 = mybir.dt.uint8
 FP8X4 = mybir.dt.float8_e4m3fn_x4
 RELU = mybir.ActivationFunctionType.Relu
-
-CHUNKS = [(0, 128), (128, 256), (256, 384), (384, 512)]
 HALF = 128
+
+CHUNK = 128
+WARM_PASSES = 8
 
 
 def tile_picked_grid_mlp_relu_sub_l_kernel(tc, xT, w1, w2, offs, out):
@@ -34,31 +35,52 @@ def tile_picked_grid_mlp_relu_sub_l_kernel(tc, xT, w1, w2, offs, out):
             tables.append(table)
         w1_rows = w1.rearrange("(p j) i -> p j i", j=4)
         w1_raw = []
-        for c, (a, b) in enumerate(CHUNKS):
-            raw = keep.tile([P, 4, b - a], F32, name=f"w1_raw{c}")
-            nc.sync.dma_start(raw[:], w1_rows[:, :, a:b])
+        for c in range(4):
+            raw = keep.tile([P, 4, CHUNK], F32, name=f"w1_raw{c}")
+            nc.sync.dma_start(raw[:], w1_rows[:, :, c * CHUNK : (c + 1) * CHUNK])
             w1_raw.append(raw)
-        w2_rows = w2.rearrange("(c t q) n -> t c q n", t=4, q=4)
-        w2_raw = keep.tile([P, 4, N], F32, name="w2_raw", tag="w2_then_h", align_bytes=64)
-        for t in range(4):
-            nc.sync.dma_start(w2_raw[:, t, :], w2_rows[t])
+        w2_rows = w2.rearrange("(p t) n -> p t n", t=4)
+        w2_raw = []
+        for u in range(2):
+            raw = keep.tile([P, 4, 128], F32, name=f"w2_raw{u}", tag=f"w2_then_h{u}", align_bytes=64)
+            nc.sync.dma_start(raw[:], w2_rows[:, :, u * 128 : (u + 1) * 128])
+            w2_raw.append(raw)
 
         x_picked = keep.tile([P, 4, V], F32, name="x_picked")
-        x_grouped = keep.tile([P, V, 4], BF16, name="x_grouped", align_bytes=64)
-        x_codes = keep.tile([P, V], U32, name="x_codes", align_bytes=64)
+        x_grouped = [
+            keep.tile([P, HALF, 4], BF16, name=f"x_grouped{half}", tag=f"x_then_w2{half}", align_bytes=64)
+            for half in range(2)
+        ]
         x_scales = keep.tile([P, V], U8, name="x_scales", align_bytes=64)
-        w1_grouped = keep.tile([P, 4, 128, 4], BF16, name="w1_grouped", align_bytes=64)
-        w1_codes = keep.tile([P, 4, 128], U32, name="w1_codes", align_bytes=64)
-        w1_scales = keep.tile([P, 4, 128], U8, name="w1_scales", align_bytes=64)
-        w2_grouped = keep.tile([P, N, 4], BF16, name="w2_grouped", align_bytes=64)
+        w1_grouped = [
+            [keep.tile([P, 2, 64, 4], BF16, name=f"w1_grouped{s}{pair}", tag=f"grouped{s}{pair}", align_bytes=64) for pair in range(2)]
+            for s in range(2)
+        ]
+        w1_codes = [keep.tile([P, 128], U32, name=f"w1_codes{t}", align_bytes=64) for t in range(4)]
+        w1_scales = [keep.tile([P, 128], U8, name=f"w1_scales{t}", align_bytes=64) for t in range(4)]
         w2_codes = keep.tile([P, N], U32, name="w2_codes", align_bytes=64)
         w2_scales = keep.tile([P, N], U8, name="w2_scales", align_bytes=64)
+        h_codes = keep.tile([P, V], U32, name="h_codes", align_bytes=64)
+        h_scales = keep.tile([P, V], U8, name="h_scales", align_bytes=64)
 
-        def w1_copy(copy, c, t0, t1):
-            a, b = CHUNKS[c]
-            dst = w1_grouped[:, t0:t1, a // 4 : b // 4, :].rearrange("p t (c q) j -> p t c j q", q=4)
-            src = w1_raw[c][:].rearrange("p j (c t q) -> p t c j q", t=4, q=4)[:, t0:t1]
+        def quantize(codes, scales, grouped):
+            nc.vector.quantize_mx(out=codes.bitcast(FP8X4), scales=scales, in_=grouped.rearrange("p c j -> p (c j)"))
+
+        def interleave(copy, grouped, planes):
+            copy(
+                out=grouped.rearrange("p (c i) t -> p c t i", i=4),
+                in_=planes.rearrange("p t (c i) -> p c t i", i=4),
+            )
+
+        def w1_copy(copy, c, pair):
+            m = slice(c % 2 * 32, (c % 2 + 1) * 32)
+            dst = w1_grouped[c // 2][pair][:, :, m, :].rearrange("p t m j -> p m j t")
+            src = w1_raw[c][:].rearrange("p j (m t) -> p m j t", t=4)[:, :, :, 2 * pair : 2 * pair + 2]
             copy(out=dst, in_=src)
+
+        def quantize_w1(t, s):
+            m = slice(s * 64, (s + 1) * 64)
+            quantize(w1_codes[t][:, m], w1_scales[t][:, m], w1_grouped[s][t // 2][:, t % 2, :, :])
 
         cols = V // 16
 
@@ -66,45 +88,16 @@ def tile_picked_grid_mlp_relu_sub_l_kernel(tc, xT, w1, w2, offs, out):
             c0, c1 = l * cols + v0 // 16, l * cols + v1 // 16
             nc.vector.tensor_copy(x_picked[:, l, v0:v1], tables[l][:].indirect(offsets[:, c0:c1]))
 
-        def x_copy(half):
-            v = slice(half * HALF, (half + 1) * HALF)
-            nc.vector.tensor_copy(
-                out=x_grouped[:, v, :].rearrange("p (c i) t -> p c t i", i=4),
-                in_=x_picked[:, :, v].rearrange("p t (c i) -> p c t i", i=4),
-            )
-
-        def quantize_x(half):
-            v = slice(half * HALF, (half + 1) * HALF)
-            nc.vector.quantize_mx(
-                out=x_codes[:, v].bitcast(FP8X4),
-                scales=x_scales[:, v],
-                in_=x_grouped[:, v, :].rearrange("p v t -> p (v t)"),
-            )
-
-        def quantize_w1(t):
-            nc.vector.quantize_mx(
-                out=w1_codes[:, t, :].bitcast(FP8X4),
-                scales=w1_scales[:, t, :],
-                in_=w1_grouped[:, t, :, :].rearrange("p m j -> p (m j)"),
-            )
-
-        def w2_copy(copy, u):
-            n = slice(u * 128, (u + 1) * 128)
-            copy(
-                out=w2_grouped[:, n, :].rearrange("p (c i) t -> p c t i", i=4),
-                in_=w2_raw[:, :, n].rearrange("p t (c i) -> p c t i", i=4),
-            )
-
+        halves = [slice(half * HALF, (half + 1) * HALF) for half in range(2)]
         hidden = [psum.tile([P, 4, HALF], F32, name=f"hidden{half}") for half in range(2)]
 
-        def mm1(t, half):
-            v = slice(half * HALF, (half + 1) * HALF)
+        def product(acc, codes, scales, moving, moving_scales):
             nc.tensor.matmul_mx(
-                out=hidden[half][:, t, :],
-                lhsT=w1_codes[:, t, :].bitcast(FP8X4),
-                lhsT_scale=w1_scales[:, t, :],
-                rhs=x_codes[:, v].bitcast(FP8X4),
-                rhs_scale=x_scales[:, v],
+                out=acc,
+                lhsT=codes.bitcast(FP8X4),
+                lhsT_scale=scales,
+                rhs=moving.bitcast(FP8X4),
+                rhs_scale=moving_scales,
                 start=True,
                 stop=True,
             )
@@ -114,52 +107,52 @@ def tile_picked_grid_mlp_relu_sub_l_kernel(tc, xT, w1, w2, offs, out):
         for half in range(2):
             gather(3, half * HALF, (half + 1) * HALF)
         for c in range(3):
-            w1_copy(nc.scalar.copy, c, 0, 4)
-        for half in range(2):
-            x_copy(half)
-        for half in range(2):
-            quantize_x(half)
-        w1_copy(nc.scalar.copy, 3, 0, 2)
-        w1_copy(nc.scalar.copy, 3, 2, 4)
+            for pair in range(2):
+                w1_copy(nc.scalar.copy, c, pair)
+        for half, v in enumerate(halves):
+            interleave(nc.vector.tensor_copy, x_grouped[half][:], x_picked[:, :, v])
+        x_codes = [keep.tile([P, HALF], U32, name="x_codes0", align_bytes=64)]
+        quantize(x_codes[0][:], x_scales[:, halves[0]], x_grouped[0][:])
+        warm = psum.tile([32, HALF], F32, name="warm")
+        for repeat in range(WARM_PASSES):
+            product(warm[:], x_codes[0][:, 0:32], x_scales[:, 0:32], x_codes[0][:], x_scales[:, halves[0]])
         for t in range(4):
-            quantize_w1(t)
-            for half in range(2):
-                mm1(t, half)
-        w2_copy(nc.scalar.copy, 0)
-        w2_copy(nc.vector.tensor_copy, 1)
-        h_codes, h_scales = [], []
-        h_both = keep.tile([P, V, 4], BF16, name="h_both", tag="w2_then_h", align_bytes=64)
-        h_grouped = [h_both[:, half * HALF : (half + 1) * HALF, :] for half in range(2)]
+            quantize_w1(t, 0)
+        for pair in range(2):
+            w1_copy(nc.vector.tensor_copy, 3, pair)
+        for t in range(4):
+            quantize_w1(t, 1)
+        x_codes.append(keep.tile([P, HALF], U32, name="x_codes1", tag="grouped10", align_bytes=64))
+        quantize(x_codes[1][:], x_scales[:, halves[1]], x_grouped[1][:])
+        for half, v in enumerate(halves):
+            for t in range(4):
+                product(hidden[half][:, t, :], w1_codes[t][:], w1_scales[t][:], x_codes[half][:], x_scales[:, v])
+        w2_grouped = [
+            keep.tile([P, 128, 4], BF16, name="w2_grouped0", align_bytes=64),
+            keep.tile([P, 128, 4], BF16, name="w2_grouped1", tag="x_then_w21", align_bytes=64),
+        ]
+        interleave(nc.scalar.copy, w2_grouped[0][:], w2_raw[0][:])
+        interleave(nc.vector.tensor_copy, w2_grouped[1][:], w2_raw[1][:])
+        for u, n in enumerate(halves):
+            quantize(w2_codes[:, n], w2_scales[:, n], w2_grouped[u][:])
+        h_grouped = []
         for half in range(2):
-            h_codes.append(keep.tile([P, HALF], U32, name=f"h_codes{half}", align_bytes=64))
-            h_scales.append(keep.tile([P, HALF], U8, name=f"h_scales{half}", align_bytes=64))
-        nc.vector.quantize_mx(
-            out=w2_codes[:].bitcast(FP8X4), scales=w2_scales[:], in_=w2_grouped[:].rearrange("p n t -> p (n t)")
-        )
-        nc.scalar.activation(h_grouped[0], hidden[0][:].rearrange("p t v -> p v t"), RELU)
-        nc.vector.tensor_scalar_max(h_grouped[1], hidden[1][:].rearrange("p t v -> p v t"), 0.0)
+            grouped = keep.tile([P, HALF, 4], BF16, name=f"h_grouped{half}", tag=f"w2_then_h{half}", align_bytes=64)
+            nc.scalar.activation(grouped[:], hidden[half][:].rearrange("p t v -> p v t"), RELU)
+            h_grouped.append(grouped)
         out_view = out.rearrange("(u p) v -> p u v", u=2)
-        for half in range(2):
-            nc.vector.quantize_mx(
-                out=h_codes[half][:].bitcast(FP8X4),
-                scales=h_scales[half][:],
-                in_=h_grouped[half].rearrange("p v t -> p (v t)"),
-            )
-            acc = psum.tile([P, 2, HALF], F32, name=f"acc{half}")
-            for u in range(2):
-                n = slice(u * 128, (u + 1) * 128)
-                nc.tensor.matmul_mx(
-                    out=acc[:, u, :],
-                    lhsT=w2_codes[:, n].bitcast(FP8X4),
-                    lhsT_scale=w2_scales[:, n],
-                    rhs=h_codes[half][:].bitcast(FP8X4),
-                    rhs_scale=h_scales[half][:],
-                    start=True,
-                    stop=True,
-                )
-            result = keep.tile([P, 2, HALF], F32, name=f"result{half}")
-            if half == 0:
-                nc.scalar.copy(result[:], acc[:])
-            else:
-                nc.vector.tensor_copy(result[:], acc[:])
-            nc.sync.dma_start(out_view[:, :, half * HALF : (half + 1) * HALF], result[:])
+        for half, v in enumerate(halves):
+            quantize(h_codes[:, v], h_scales[:, v], h_grouped[half][:])
+        acc0 = psum.tile([P, 2, HALF], F32, name="acc0")
+        for u, n in enumerate(halves):
+            product(acc0[:, u, :], w2_codes[:, n], w2_scales[:, n], h_codes[:, halves[0]], h_scales[:, halves[0]])
+        result0 = keep.tile([P, 2, HALF], F32, name="result0")
+        nc.vector.tensor_copy(result0[:], acc0[:])
+        nc.sync.dma_start(out_view[:, :, halves[0]], result0[:])
+        result1 = keep.tile([P, 2, HALF], F32, name="result1")
+        for u, n in enumerate(halves):
+            acc = psum.tile([P, HALF], F32, name=f"acc1{u}")
+            product(acc[:], w2_codes[:, n], w2_scales[:, n], h_codes[:, halves[1]], h_scales[:, halves[1]])
+            copy = nc.scalar.copy if u == 0 else nc.vector.tensor_copy
+            copy(result1[:, u, :], acc[:])
+        nc.sync.dma_start(out_view[:, :, halves[1]], result1[:])

@@ -16,7 +16,7 @@ RELU = mybir.ActivationFunctionType.Relu
 HALF = 128
 
 CHUNK = 128
-WARM_PASSES = 8
+WARM_PASSES = 12
 
 
 def tile_picked_grid_mlp_relu_sub_l_kernel(tc, xT, w1, w2, offs, out):
@@ -46,7 +46,7 @@ def tile_picked_grid_mlp_relu_sub_l_kernel(tc, xT, w1, w2, offs, out):
             nc.sync.dma_start(raw[:], w2_rows[:, :, u * 128 : (u + 1) * 128])
             w2_raw.append(raw)
 
-        x_picked = keep.tile([P, 4, V], F32, name="x_picked")
+        x_picked = keep.tile([P, 4, V], F32, name="x_picked", align_bytes=64)
         x_grouped = [
             keep.tile([P, HALF, 4], BF16, name=f"x_grouped{half}", tag=f"x_then_w2{half}", align_bytes=64)
             for half in range(2)
@@ -89,7 +89,8 @@ def tile_picked_grid_mlp_relu_sub_l_kernel(tc, xT, w1, w2, offs, out):
             nc.vector.tensor_copy(x_picked[:, l, v0:v1], tables[l][:].indirect(offsets[:, c0:c1]))
 
         halves = [slice(half * HALF, (half + 1) * HALF) for half in range(2)]
-        hidden = [psum.tile([P, 4, HALF], F32, name=f"hidden{half}") for half in range(2)]
+        groups = [(0, 0, HALF), (1, 0, 64), (1, 64, HALF)]
+        hidden = [psum.tile([P, 4, b - a], F32, name=f"hidden{half}_{a}") for half, a, b in groups]
 
         def product(acc, codes, scales, moving, moving_scales):
             nc.tensor.matmul_mx(
@@ -102,8 +103,13 @@ def tile_picked_grid_mlp_relu_sub_l_kernel(tc, xT, w1, w2, offs, out):
                 stop=True,
             )
 
+        warm_values = x_picked[:, 3, :].bitcast(BF16)
+        warm_codes = keep.tile([P, HALF], U32, name="warm_codes", align_bytes=64)
+        warm_scales = keep.tile([P, HALF], U8, name="warm_scales", align_bytes=64)
+        nc.scalar.copy(warm_values, tables[1][:])
         for l in range(3):
             gather(l, 0, V)
+        quantize(warm_codes[:], warm_scales[:], warm_values.rearrange("p (c j) -> p c j", j=4))
         for half in range(2):
             gather(3, half * HALF, (half + 1) * HALF)
         for c in range(3):
@@ -115,7 +121,7 @@ def tile_picked_grid_mlp_relu_sub_l_kernel(tc, xT, w1, w2, offs, out):
         quantize(x_codes[0][:], x_scales[:, halves[0]], x_grouped[0][:])
         warm = psum.tile([32, HALF], F32, name="warm")
         for repeat in range(WARM_PASSES):
-            product(warm[:], x_codes[0][:, 0:32], x_scales[:, 0:32], x_codes[0][:], x_scales[:, halves[0]])
+            product(warm[:], warm_codes[:, 0:32], warm_scales[:, 0:32], warm_codes[:], warm_scales[:])
         for t in range(4):
             quantize_w1(t, 0)
         for pair in range(2):
@@ -124,9 +130,10 @@ def tile_picked_grid_mlp_relu_sub_l_kernel(tc, xT, w1, w2, offs, out):
             quantize_w1(t, 1)
         x_codes.append(keep.tile([P, HALF], U32, name="x_codes1", tag="grouped10", align_bytes=64))
         quantize(x_codes[1][:], x_scales[:, halves[1]], x_grouped[1][:])
-        for half, v in enumerate(halves):
+        for g, (half, a, b) in enumerate(groups):
+            v = slice(half * HALF + a, half * HALF + b)
             for t in range(4):
-                product(hidden[half][:, t, :], w1_codes[t][:], w1_scales[t][:], x_codes[half][:], x_scales[:, v])
+                product(hidden[g][:, t, :], w1_codes[t][:], w1_scales[t][:], x_codes[half][:, a:b], x_scales[:, v])
         w2_grouped = [
             keep.tile([P, 128, 4], BF16, name="w2_grouped0", align_bytes=64),
             keep.tile([P, 128, 4], BF16, name="w2_grouped1", tag="x_then_w21", align_bytes=64),
@@ -138,8 +145,10 @@ def tile_picked_grid_mlp_relu_sub_l_kernel(tc, xT, w1, w2, offs, out):
         h_grouped = []
         for half in range(2):
             grouped = keep.tile([P, HALF, 4], BF16, name=f"h_grouped{half}", tag=f"w2_then_h{half}", align_bytes=64)
-            nc.scalar.activation(grouped[:], hidden[half][:].rearrange("p t v -> p v t"), RELU)
             h_grouped.append(grouped)
+        nc.scalar.activation(h_grouped[0][:], hidden[0][:].rearrange("p t v -> p v t"), RELU)
+        nc.vector.tensor_scalar_max(h_grouped[1][:, 0:64, :], hidden[1][:].rearrange("p t v -> p v t"), 0.0)
+        nc.scalar.activation(h_grouped[1][:, 64:HALF, :], hidden[2][:].rearrange("p t v -> p v t"), RELU)
         out_view = out.rearrange("(u p) v -> p u v", u=2)
         for half, v in enumerate(halves):
             quantize(h_codes[:, v], h_scales[:, v], h_grouped[half][:])

@@ -30,7 +30,7 @@ def tile_picked_grid_mlp_relu_sub_l_kernel(tc, xT, w1, w2, offs, out):
         x_rows = xT.rearrange("(p l) w -> p l w", l=4)
         tables = []
         for l in range(4):
-            table = keep.tile([P, T], F32, name=f"table{l}")
+            table = keep.tile([P, T], F32, name=f"table{l}", tag=f"table{l}", align_bytes=64)
             nc.sync.dma_start(table[:], x_rows[:, l, :])
             tables.append(table)
         w1_rows = w1.rearrange("(p j) i -> p j i", j=4)
@@ -42,13 +42,14 @@ def tile_picked_grid_mlp_relu_sub_l_kernel(tc, xT, w1, w2, offs, out):
         w2_rows = w2.rearrange("(p t) n -> p t n", t=4)
         w2_raw = []
         for u in range(2):
+            n = slice(u * 128, (u + 1) * 128)
             raw = keep.tile([P, 4, 128], F32, name=f"w2_raw{u}", tag=f"w2_then_h{u}", align_bytes=64)
-            nc.sync.dma_start(raw[:], w2_rows[:, :, u * 128 : (u + 1) * 128])
+            nc.sync.dma_start(raw[:], w2_rows[:, :, n])
             w2_raw.append(raw)
 
         x_picked = keep.tile([P, 4, V], F32, name="x_picked", align_bytes=64)
         x_grouped = [
-            keep.tile([P, HALF, 4], BF16, name=f"x_grouped{half}", tag=f"x_then_w2{half}", align_bytes=64)
+            keep.tile([P, HALF, 4], BF16, name=f"x_grouped{half}", align_bytes=64)
             for half in range(2)
         ]
         x_scales = keep.tile([P, V], U8, name="x_scales", align_bytes=64)
@@ -89,8 +90,7 @@ def tile_picked_grid_mlp_relu_sub_l_kernel(tc, xT, w1, w2, offs, out):
             nc.vector.tensor_copy(x_picked[:, l, v0:v1], tables[l][:].indirect(offsets[:, c0:c1]))
 
         halves = [slice(half * HALF, (half + 1) * HALF) for half in range(2)]
-        groups = [(0, 0, HALF), (1, 0, 64), (1, 64, HALF)]
-        hidden = [psum.tile([P, 4, b - a], F32, name=f"hidden{half}_{a}") for half, a, b in groups]
+        hidden = [psum.tile([P, 4, HALF], F32, name=f"hidden{half}") for half in range(2)]
 
         def product(acc, codes, scales, moving, moving_scales):
             nc.tensor.matmul_mx(
@@ -103,13 +103,18 @@ def tile_picked_grid_mlp_relu_sub_l_kernel(tc, xT, w1, w2, offs, out):
                 stop=True,
             )
 
-        warm_values = x_picked[:, 3, :].bitcast(BF16)
+        warm_seed = keep.tile([P, 64], BF16, name="warm_seed")
+        warm_values = keep.tile([P, HALF, 4], BF16, name="warm_values", align_bytes=64)
         warm_codes = keep.tile([P, HALF], U32, name="warm_codes", align_bytes=64)
         warm_scales = keep.tile([P, HALF], U8, name="warm_scales", align_bytes=64)
-        nc.scalar.copy(warm_values, tables[1][:])
+        nc.vector.memset(warm_seed[:], 1.0)
+        nc.vector.memset(warm_values[:, 16:, :], 1.0)
+        nc.scalar.activation(warm_values[:, 0:16, :].rearrange("p c j -> p (c j)"), warm_seed[:], RELU)
+        quantize(warm_codes[:], warm_scales[:], warm_values[:])
         for l in range(3):
             gather(l, 0, V)
-        quantize(warm_codes[:], warm_scales[:], warm_values.rearrange("p (c j) -> p c j", j=4))
+        warm_weights = keep.tile([P, 32], U32, name="warm_weights", tag="table2", align_bytes=64)
+        nc.gpsimd.tensor_copy(warm_weights[:], warm_codes[:, 0:32])
         for half in range(2):
             gather(3, half * HALF, (half + 1) * HALF)
         for c in range(3):
@@ -117,51 +122,40 @@ def tile_picked_grid_mlp_relu_sub_l_kernel(tc, xT, w1, w2, offs, out):
                 w1_copy(nc.scalar.copy, c, pair)
         for half, v in enumerate(halves):
             interleave(nc.vector.tensor_copy, x_grouped[half][:], x_picked[:, :, v])
-        x_codes = [keep.tile([P, HALF], U32, name="x_codes0", align_bytes=64)]
-        quantize(x_codes[0][:], x_scales[:, halves[0]], x_grouped[0][:])
+        x_codes = keep.tile([P, V], U32, name="x_codes", align_bytes=64)
+        for half, v in enumerate(halves):
+            quantize(x_codes[:, v], x_scales[:, v], x_grouped[half][:])
         warm = psum.tile([32, HALF], F32, name="warm")
         for repeat in range(WARM_PASSES):
-            product(warm[:], warm_codes[:, 0:32], warm_scales[:, 0:32], warm_codes[:], warm_scales[:])
+            product(warm[:], warm_weights[:], warm_scales[:, 0:32], warm_codes[:], warm_scales[:])
         for t in range(4):
             quantize_w1(t, 0)
         for pair in range(2):
             w1_copy(nc.vector.tensor_copy, 3, pair)
         for t in range(4):
             quantize_w1(t, 1)
-        x_codes.append(keep.tile([P, HALF], U32, name="x_codes1", tag="grouped10", align_bytes=64))
-        quantize(x_codes[1][:], x_scales[:, halves[1]], x_grouped[1][:])
-        for g, (half, a, b) in enumerate(groups):
-            v = slice(half * HALF + a, half * HALF + b)
-            for t in range(4):
-                product(hidden[g][:, t, :], w1_codes[t][:], w1_scales[t][:], x_codes[half][:, a:b], x_scales[:, v])
-        w2_grouped = [
-            keep.tile([P, 128, 4], BF16, name="w2_grouped0", align_bytes=64),
-            keep.tile([P, 128, 4], BF16, name="w2_grouped1", tag="x_then_w21", align_bytes=64),
-        ]
+        for t in range(4):
+            for half, v in enumerate(halves):
+                product(hidden[half][:, t, :], w1_codes[t][:], w1_scales[t][:], x_codes[:, v], x_scales[:, v])
+        w2_grouped = [keep.tile([P, 128, 4], BF16, name=f"w2_grouped{u}", align_bytes=64) for u in range(2)]
         interleave(nc.scalar.copy, w2_grouped[0][:], w2_raw[0][:])
         interleave(nc.vector.tensor_copy, w2_grouped[1][:], w2_raw[1][:])
         for u, n in enumerate(halves):
             quantize(w2_codes[:, n], w2_scales[:, n], w2_grouped[u][:])
-        h_grouped = []
-        for half in range(2):
-            grouped = keep.tile([P, HALF, 4], BF16, name=f"h_grouped{half}", tag=f"w2_then_h{half}", align_bytes=64)
-            h_grouped.append(grouped)
+        h_grouped = [
+            keep.tile([P, HALF, 4], BF16, name=f"h_grouped{half}", tag=f"w2_then_h{half}", align_bytes=64)
+            for half in range(2)
+        ]
         nc.scalar.activation(h_grouped[0][:], hidden[0][:].rearrange("p t v -> p v t"), RELU)
-        nc.vector.tensor_scalar_max(h_grouped[1][:, 0:64, :], hidden[1][:].rearrange("p t v -> p v t"), 0.0)
-        nc.scalar.activation(h_grouped[1][:, 64:HALF, :], hidden[2][:].rearrange("p t v -> p v t"), RELU)
-        out_view = out.rearrange("(u p) v -> p u v", u=2)
+        nc.vector.tensor_scalar_max(h_grouped[1][:], hidden[1][:].rearrange("p t v -> p v t"), 0.0)
         for half, v in enumerate(halves):
             quantize(h_codes[:, v], h_scales[:, v], h_grouped[half][:])
-        acc0 = psum.tile([P, 2, HALF], F32, name="acc0")
-        for u, n in enumerate(halves):
-            product(acc0[:, u, :], w2_codes[:, n], w2_scales[:, n], h_codes[:, halves[0]], h_scales[:, halves[0]])
-        result0 = keep.tile([P, 2, HALF], F32, name="result0")
-        nc.vector.tensor_copy(result0[:], acc0[:])
-        nc.sync.dma_start(out_view[:, :, halves[0]], result0[:])
-        result1 = keep.tile([P, 2, HALF], F32, name="result1")
-        for u, n in enumerate(halves):
-            acc = psum.tile([P, HALF], F32, name=f"acc1{u}")
-            product(acc[:], w2_codes[:, n], w2_scales[:, n], h_codes[:, halves[1]], h_scales[:, halves[1]])
-            copy = nc.scalar.copy if u == 0 else nc.vector.tensor_copy
-            copy(result1[:, u, :], acc[:])
-        nc.sync.dma_start(out_view[:, :, halves[1]], result1[:])
+        out_view = out.rearrange("(u p) v -> p u v", u=2)
+        for half, v in enumerate(halves):
+            result = keep.tile([P, 2, HALF], F32, name=f"result{half}")
+            for u, n in enumerate(halves):
+                acc = psum.tile([P, HALF], F32, name=f"acc{half}{u}")
+                product(acc[:], w2_codes[:, n], w2_scales[:, n], h_codes[:, v], h_scales[:, v])
+                copy = nc.scalar.copy if u == 0 else nc.vector.tensor_copy
+                copy(result[:, u, :], acc[:])
+            nc.sync.dma_start(out_view[:, :, v], result[:])

@@ -30,7 +30,7 @@ def tile_picked_grid_mlp_relu_sub_l_kernel(tc, xT, w1, w2, offs, out):
         x_rows = xT.rearrange("(p l) w -> p l w", l=4)
         tables = []
         for l in range(4):
-            table = keep.tile([P, T], F32, name=f"table{l}", tag=f"table{l}", align_bytes=64)
+            table = keep.tile([P, T], F32, name=f"table{l}")
             nc.sync.dma_start(table[:], x_rows[:, l, :])
             tables.append(table)
         w1_rows = w1.rearrange("(p j) i -> p j i", j=4)
@@ -108,15 +108,13 @@ def tile_picked_grid_mlp_relu_sub_l_kernel(tc, xT, w1, w2, offs, out):
         warm_codes = keep.tile([P, HALF], U32, name="warm_codes", align_bytes=64)
         warm_scales = keep.tile([P, HALF], U8, name="warm_scales", align_bytes=64)
         nc.vector.memset(warm_seed[:], 1.0)
-        nc.vector.memset(warm_values[:, 16:, :], 1.0)
         nc.scalar.activation(warm_values[:, 0:16, :].rearrange("p c j -> p (c j)"), warm_seed[:], RELU)
-        quantize(warm_codes[:], warm_scales[:], warm_values[:])
+        nc.scalar.copy(warm_values[:, 16:, :].rearrange("p c j -> p (c j)"), tables[2][:, 64:])
         for l in range(3):
             gather(l, 0, V)
-        warm_weights = keep.tile([P, 32], U32, name="warm_weights", tag="table2", align_bytes=64)
-        nc.gpsimd.tensor_copy(warm_weights[:], warm_codes[:, 0:32])
         for half in range(2):
             gather(3, half * HALF, (half + 1) * HALF)
+        quantize(warm_codes[:], warm_scales[:], warm_values[:])
         for c in range(3):
             for pair in range(2):
                 w1_copy(nc.scalar.copy, c, pair)
@@ -127,7 +125,7 @@ def tile_picked_grid_mlp_relu_sub_l_kernel(tc, xT, w1, w2, offs, out):
             quantize(x_codes[:, v], x_scales[:, v], x_grouped[half][:])
         warm = psum.tile([32, HALF], F32, name="warm")
         for repeat in range(WARM_PASSES):
-            product(warm[:], warm_weights[:], warm_scales[:, 0:32], warm_codes[:], warm_scales[:])
+            product(warm[:], warm_codes[:, 0:32], warm_scales[:, 0:32], warm_codes[:], warm_scales[:])
         for t in range(4):
             quantize_w1(t, 0)
         for pair in range(2):

@@ -13,6 +13,7 @@ U16 = mybir.dt.uint16
 U8 = mybir.dt.uint8
 FP8X4 = mybir.dt.float8_e4m3fn_x4
 RELU = mybir.ActivationFunctionType.Relu
+COPY = mybir.ActivationFunctionType.Copy
 HALF = 128
 
 CHUNK = 128
@@ -47,7 +48,7 @@ def tile_picked_grid_mlp_relu_sub_l_kernel(tc, xT, w1, w2, offs, out):
             nc.sync.dma_start(raw[:], w2_rows[:, :, n])
             w2_raw.append(raw)
 
-        x_picked = keep.tile([P, 4, V], F32, name="x_picked", align_bytes=64)
+        x_picked = keep.tile([P, 4, V], BF16, name="x_picked", align_bytes=64)
         x_grouped = [
             keep.tile([P, HALF, 4], BF16, name=f"x_grouped{half}", align_bytes=64)
             for half in range(2)
@@ -61,7 +62,6 @@ def tile_picked_grid_mlp_relu_sub_l_kernel(tc, xT, w1, w2, offs, out):
         w1_scales = [keep.tile([P, 128], U8, name=f"w1_scales{t}", align_bytes=64) for t in range(4)]
         w2_codes = keep.tile([P, N], U32, name="w2_codes", align_bytes=64)
         w2_scales = keep.tile([P, N], U8, name="w2_scales", align_bytes=64)
-        h_codes = keep.tile([P, V], U32, name="h_codes", align_bytes=64)
         h_scales = keep.tile([P, V], U8, name="h_scales", align_bytes=64)
 
         def quantize(codes, scales, grouped):
@@ -103,57 +103,66 @@ def tile_picked_grid_mlp_relu_sub_l_kernel(tc, xT, w1, w2, offs, out):
                 stop=True,
             )
 
-        warm_seed = keep.tile([P, 64], BF16, name="warm_seed")
         warm_values = keep.tile([P, HALF, 4], BF16, name="warm_values", align_bytes=64)
         warm_codes = keep.tile([P, HALF], U32, name="warm_codes", align_bytes=64)
         warm_scales = keep.tile([P, HALF], U8, name="warm_scales", align_bytes=64)
-        nc.vector.memset(warm_seed[:], 1.0)
-        nc.scalar.activation(warm_values[:, 0:16, :].rearrange("p c j -> p (c j)"), warm_seed[:], RELU)
-        nc.scalar.copy(warm_values[:, 16:, :].rearrange("p c j -> p (c j)"), tables[2][:, 64:])
-        for l in range(3):
+        warm_weights = keep.tile([P, 32], U32, name="warm_weights", align_bytes=64)
+        warm_weight_scales = keep.tile([P, 32], U8, name="warm_weight_scales", align_bytes=64)
+        nc.vector.memset(warm_values[:], 1.0)
+        quantize(warm_codes[:], warm_scales[:], warm_values[:])
+        table0_rounded = keep.tile([P, T], BF16, name="table0_rounded", align_bytes=64)
+        nc.scalar.copy(table0_rounded[:], tables[0][:])
+        nc.scalar.activation(x_picked[:, 0, :], table0_rounded[:].indirect(offsets[:, 0:cols]), COPY)
+        for l in range(1, 3):
             gather(l, 0, V)
         for half in range(2):
             gather(3, half * HALF, (half + 1) * HALF)
-        quantize(warm_codes[:], warm_scales[:], warm_values[:])
+        quantize(warm_weights[:], warm_weight_scales[:], table0_rounded[:, 0:128].rearrange("p (c j) -> p c j", j=4))
         for c in range(3):
             for pair in range(2):
                 w1_copy(nc.scalar.copy, c, pair)
         for half, v in enumerate(halves):
             interleave(nc.vector.tensor_copy, x_grouped[half][:], x_picked[:, :, v])
-        x_codes = keep.tile([P, V], U32, name="x_codes", align_bytes=64)
-        for half, v in enumerate(halves):
-            quantize(x_codes[:, v], x_scales[:, v], x_grouped[half][:])
+        x_codes = [keep.tile([P, HALF], U32, name="x_codes0", align_bytes=64)]
+        quantize(x_codes[0][:], x_scales[:, halves[0]], x_grouped[0][:])
         warm = psum.tile([32, HALF], F32, name="warm")
         for repeat in range(WARM_PASSES):
-            product(warm[:], warm_codes[:, 0:32], warm_scales[:, 0:32], warm_codes[:], warm_scales[:])
+            product(warm[:], warm_weights[:], warm_weight_scales[:], warm_codes[:], warm_scales[:])
         for t in range(4):
             quantize_w1(t, 0)
         for pair in range(2):
             w1_copy(nc.vector.tensor_copy, 3, pair)
         for t in range(4):
             quantize_w1(t, 1)
-        for t in range(4):
-            for half, v in enumerate(halves):
-                product(hidden[half][:, t, :], w1_codes[t][:], w1_scales[t][:], x_codes[:, v], x_scales[:, v])
-        w2_grouped = [keep.tile([P, 128, 4], BF16, name=f"w2_grouped{u}", align_bytes=64) for u in range(2)]
+        x_codes.append(keep.tile([P, HALF], U32, name="x_codes1", tag="grouped10", align_bytes=64))
+        quantize(x_codes[1][:], x_scales[:, halves[1]], x_grouped[1][:])
+        for half, v in enumerate(halves):
+            for t in range(4):
+                product(hidden[half][:, t, :], w1_codes[t][:], w1_scales[t][:], x_codes[half][:], x_scales[:, v])
+        w2_grouped = [keep.tile([P, 128, 4], BF16, name=f"w2_grouped{u}", tag=f"w2_grouped{u}", align_bytes=64) for u in range(2)]
         interleave(nc.scalar.copy, w2_grouped[0][:], w2_raw[0][:])
-        interleave(nc.vector.tensor_copy, w2_grouped[1][:], w2_raw[1][:])
-        for u, n in enumerate(halves):
-            quantize(w2_codes[:, n], w2_scales[:, n], w2_grouped[u][:])
+        interleave(nc.scalar.copy, w2_grouped[1][:, 0:64, :], w2_raw[1][:, :, 0:64])
+        interleave(nc.vector.tensor_copy, w2_grouped[1][:, 64:128, :], w2_raw[1][:, :, 64:128])
+        quantize(w2_codes[:, halves[0]], w2_scales[:, halves[0]], w2_grouped[0][:])
         h_grouped = [
-            keep.tile([P, HALF, 4], BF16, name=f"h_grouped{half}", tag=f"w2_then_h{half}", align_bytes=64)
+            keep.tile([P, HALF, 4], BF16, name=f"h_grouped{half}", tag=f"w2_then_h{1 - half}", align_bytes=64)
             for half in range(2)
         ]
-        nc.scalar.activation(h_grouped[0][:], hidden[0][:].rearrange("p t v -> p v t"), RELU)
-        nc.vector.tensor_scalar_max(h_grouped[1][:], hidden[1][:].rearrange("p t v -> p v t"), 0.0)
+        nc.vector.tensor_scalar_max(h_grouped[0][:], hidden[0][:].rearrange("p t v -> p v t"), 0.0)
+        nc.scalar.activation(h_grouped[1][:], hidden[1][:].rearrange("p t v -> p v t"), RELU)
+        quantize(w2_codes[:, halves[1]], w2_scales[:, halves[1]], w2_grouped[1][:])
+        h_codes = [
+            keep.tile([P, HALF], U32, name="h_codes0", align_bytes=64),
+            keep.tile([P, HALF], U32, name="h_codes1", tag="w2_grouped1", align_bytes=64),
+        ]
         for half, v in enumerate(halves):
-            quantize(h_codes[:, v], h_scales[:, v], h_grouped[half][:])
+            quantize(h_codes[half][:], h_scales[:, v], h_grouped[half][:])
         out_view = out.rearrange("(u p) v -> p u v", u=2)
         for half, v in enumerate(halves):
             result = keep.tile([P, 2, HALF], F32, name=f"result{half}")
             for u, n in enumerate(halves):
                 acc = psum.tile([P, HALF], F32, name=f"acc{half}{u}")
-                product(acc[:], w2_codes[:, n], w2_scales[:, n], h_codes[:, v], h_scales[:, v])
+                product(acc[:], w2_codes[:, n], w2_scales[:, n], h_codes[half][:], h_scales[:, v])
                 copy = nc.scalar.copy if u == 0 else nc.vector.tensor_copy
                 copy(result[:, u, :], acc[:])
             nc.sync.dma_start(out_view[:, :, v], result[:])

@@ -108,16 +108,21 @@ def tile_picked_grid_mlp_relu_sub_l_kernel(tc, xT, w1, w2, offs, out):
         warm_scales = keep.tile([P, HALF], U8, name="warm_scales", align_bytes=64)
         warm_weights = keep.tile([P, 32], U32, name="warm_weights", align_bytes=64)
         warm_weight_scales = keep.tile([P, 32], U8, name="warm_weight_scales", align_bytes=64)
-        nc.vector.memset(warm_values[:], 1.0)
+        warm_seed = keep.tile([P, 64], BF16, name="warm_seed")
+        warm_weight_values = keep.tile([P, 32, 4], BF16, name="warm_weight_values", align_bytes=64)
+        nc.vector.memset(warm_seed[:], 1.0)
+        nc.vector.memset(warm_values[:, 16:, :], 1.0)
+        nc.scalar.activation(warm_values[:, 0:16, :].rearrange("p c j -> p (c j)"), warm_seed[:], RELU)
         quantize(warm_codes[:], warm_scales[:], warm_values[:])
         table0_rounded = keep.tile([P, T], BF16, name="table0_rounded", align_bytes=64)
         nc.scalar.copy(table0_rounded[:], tables[0][:])
         nc.scalar.activation(x_picked[:, 0, :], table0_rounded[:].indirect(offsets[:, 0:cols]), COPY)
+        nc.scalar.copy(warm_weight_values[:].rearrange("p c j -> p (c j)"), tables[2][:, 0:128])
         for l in range(1, 3):
             gather(l, 0, V)
+        quantize(warm_weights[:], warm_weight_scales[:], warm_weight_values[:])
         for half in range(2):
             gather(3, half * HALF, (half + 1) * HALF)
-        quantize(warm_weights[:], warm_weight_scales[:], table0_rounded[:, 0:128].rearrange("p (c j) -> p c j", j=4))
         for c in range(3):
             for pair in range(2):
                 w1_copy(nc.scalar.copy, c, pair)

@@ -50,7 +50,7 @@ def tile_picked_grid_mlp_relu_sub_l_kernel(tc, xT, w1, w2, offs, out):
 
         x_picked = keep.tile([P, 4, V], BF16, name="x_picked", align_bytes=64)
         x_grouped = [
-            keep.tile([P, HALF, 4], BF16, name=f"x_grouped{half}", align_bytes=64)
+            keep.tile([P, HALF, 4], BF16, name=f"x_grouped{half}", tag=f"x_then_w2{half}", align_bytes=64)
             for half in range(2)
         ]
         x_scales = keep.tile([P, V], U8, name="x_scales", align_bytes=64)
@@ -62,6 +62,7 @@ def tile_picked_grid_mlp_relu_sub_l_kernel(tc, xT, w1, w2, offs, out):
         w1_scales = [keep.tile([P, 128], U8, name=f"w1_scales{t}", align_bytes=64) for t in range(4)]
         w2_codes = keep.tile([P, N], U32, name="w2_codes", align_bytes=64)
         w2_scales = keep.tile([P, N], U8, name="w2_scales", align_bytes=64)
+        h_codes = keep.tile([P, V], U32, name="h_codes", align_bytes=64)
         h_scales = keep.tile([P, V], U8, name="h_scales", align_bytes=64)
 
         def quantize(codes, scales, grouped):
@@ -90,7 +91,8 @@ def tile_picked_grid_mlp_relu_sub_l_kernel(tc, xT, w1, w2, offs, out):
             nc.vector.tensor_copy(x_picked[:, l, v0:v1], tables[l][:].indirect(offsets[:, c0:c1]))
 
         halves = [slice(half * HALF, (half + 1) * HALF) for half in range(2)]
-        hidden = [psum.tile([P, 4, HALF], F32, name=f"hidden{half}") for half in range(2)]
+        groups = [(0, 0, HALF), (1, 0, 64), (1, 64, HALF)]
+        hidden = [psum.tile([P, 4, b - a], F32, name=f"hidden{half}_{a}") for half, a, b in groups]
 
         def product(acc, codes, scales, moving, moving_scales):
             nc.tensor.matmul_mx(
@@ -141,33 +143,38 @@ def tile_picked_grid_mlp_relu_sub_l_kernel(tc, xT, w1, w2, offs, out):
             quantize_w1(t, 1)
         x_codes.append(keep.tile([P, HALF], U32, name="x_codes1", tag="grouped10", align_bytes=64))
         quantize(x_codes[1][:], x_scales[:, halves[1]], x_grouped[1][:])
-        for half, v in enumerate(halves):
+        for g, (half, a, b) in enumerate(groups):
+            v = slice(half * HALF + a, half * HALF + b)
             for t in range(4):
-                product(hidden[half][:, t, :], w1_codes[t][:], w1_scales[t][:], x_codes[half][:], x_scales[:, v])
-        w2_grouped = [keep.tile([P, 128, 4], BF16, name=f"w2_grouped{u}", tag=f"w2_grouped{u}", align_bytes=64) for u in range(2)]
+                product(hidden[g][:, t, :], w1_codes[t][:], w1_scales[t][:], x_codes[half][:, a:b], x_scales[:, v])
+        w2_grouped = [
+            keep.tile([P, 128, 4], BF16, name="w2_grouped0", align_bytes=64),
+            keep.tile([P, 128, 4], BF16, name="w2_grouped1", tag="x_then_w21", align_bytes=64),
+        ]
         interleave(nc.scalar.copy, w2_grouped[0][:], w2_raw[0][:])
-        interleave(nc.scalar.copy, w2_grouped[1][:, 0:64, :], w2_raw[1][:, :, 0:64])
-        interleave(nc.vector.tensor_copy, w2_grouped[1][:, 64:128, :], w2_raw[1][:, :, 64:128])
-        quantize(w2_codes[:, halves[0]], w2_scales[:, halves[0]], w2_grouped[0][:])
-        h_grouped = [
-            keep.tile([P, HALF, 4], BF16, name=f"h_grouped{half}", tag=f"w2_then_h{1 - half}", align_bytes=64)
-            for half in range(2)
-        ]
-        nc.vector.tensor_scalar_max(h_grouped[0][:], hidden[0][:].rearrange("p t v -> p v t"), 0.0)
-        nc.scalar.activation(h_grouped[1][:], hidden[1][:].rearrange("p t v -> p v t"), RELU)
-        quantize(w2_codes[:, halves[1]], w2_scales[:, halves[1]], w2_grouped[1][:])
-        h_codes = [
-            keep.tile([P, HALF], U32, name="h_codes0", align_bytes=64),
-            keep.tile([P, HALF], U32, name="h_codes1", tag="w2_grouped1", align_bytes=64),
-        ]
-        for half, v in enumerate(halves):
-            quantize(h_codes[half][:], h_scales[:, v], h_grouped[half][:])
+        interleave(nc.vector.tensor_copy, w2_grouped[1][:], w2_raw[1][:])
+        for u, n in enumerate(halves):
+            quantize(w2_codes[:, n], w2_scales[:, n], w2_grouped[u][:])
+        h_grouped = []
+        for half in range(2):
+            grouped = keep.tile([P, HALF, 4], BF16, name=f"h_grouped{half}", tag=f"w2_then_h{half}", align_bytes=64)
+            h_grouped.append(grouped)
+        nc.scalar.activation(h_grouped[0][:], hidden[0][:].rearrange("p t v -> p v t"), RELU)
+        nc.vector.tensor_scalar_max(h_grouped[1][:, 0:64, :], hidden[1][:].rearrange("p t v -> p v t"), 0.0)
+        nc.scalar.activation(h_grouped[1][:, 64:HALF, :], hidden[2][:].rearrange("p t v -> p v t"), RELU)
         out_view = out.rearrange("(u p) v -> p u v", u=2)
         for half, v in enumerate(halves):
-            result = keep.tile([P, 2, HALF], F32, name=f"result{half}")
-            for u, n in enumerate(halves):
-                acc = psum.tile([P, HALF], F32, name=f"acc{half}{u}")
-                product(acc[:], w2_codes[:, n], w2_scales[:, n], h_codes[half][:], h_scales[:, v])
-                copy = nc.scalar.copy if u == 0 else nc.vector.tensor_copy
-                copy(result[:, u, :], acc[:])
-            nc.sync.dma_start(out_view[:, :, v], result[:])
+            quantize(h_codes[:, v], h_scales[:, v], h_grouped[half][:])
+        acc0 = psum.tile([P, 2, HALF], F32, name="acc0")
+        for u, n in enumerate(halves):
+            product(acc0[:, u, :], w2_codes[:, n], w2_scales[:, n], h_codes[:, halves[0]], h_scales[:, halves[0]])
+        result0 = keep.tile([P, 2, HALF], F32, name="result0")
+        nc.vector.tensor_copy(result0[:], acc0[:])
+        nc.sync.dma_start(out_view[:, :, halves[0]], result0[:])
+        result1 = keep.tile([P, 2, HALF], F32, name="result1")
+        for u, n in enumerate(halves):
+            acc = psum.tile([P, HALF], F32, name=f"acc1{u}")
+            product(acc[:], w2_codes[:, n], w2_scales[:, n], h_codes[:, halves[1]], h_scales[:, halves[1]])
+            copy = nc.scalar.copy if u == 0 else nc.vector.tensor_copy
+            copy(result1[:, u, :], acc[:])
+        nc.sync.dma_start(out_view[:, :, halves[1]], result1[:])

@@ -27,13 +27,14 @@ def tile_picked_grid_mlp_relu_sub_l_kernel(tc, xT, w1, w2, offs, out):
         psum = ctx.enter_context(tc.psum_pool(name="psum", bufs=1))
 
         offsets = keep.tile([P, D * V // 16], U16, name="offsets")
-        nc.sync.dma_start(offsets[:], offs)
         x_rows = xT.rearrange("(p l) w -> p l w", l=4)
         tables = []
         for l in range(4):
             table = keep.tile([P, T], F32, name=f"table{l}")
             nc.sync.dma_start(table[:], x_rows[:, l, :])
             tables.append(table)
+            if l == 0:
+                nc.sync.dma_start(offsets[:], offs)
         w1_rows = w1.rearrange("(p j) i -> p j i", j=4)
         w1_raw = []
         for c in range(4):
@@ -111,7 +112,6 @@ def tile_picked_grid_mlp_relu_sub_l_kernel(tc, xT, w1, w2, offs, out):
         warm_weights = keep.tile([P, 32], U32, name="warm_weights", align_bytes=64)
         warm_weight_scales = keep.tile([P, 32], U8, name="warm_weight_scales", align_bytes=64)
         warm_seed = keep.tile([P, 64], BF16, name="warm_seed")
-        warm_weight_values = keep.tile([P, 32, 4], BF16, name="warm_weight_values", align_bytes=64)
         nc.vector.memset(warm_seed[:], 1.0)
         nc.vector.memset(warm_values[:, 16:, :], 1.0)
         nc.scalar.activation(warm_values[:, 0:16, :].rearrange("p c j -> p (c j)"), warm_seed[:], RELU)
@@ -119,12 +119,11 @@ def tile_picked_grid_mlp_relu_sub_l_kernel(tc, xT, w1, w2, offs, out):
         table0_rounded = keep.tile([P, T], BF16, name="table0_rounded", align_bytes=64)
         nc.scalar.copy(table0_rounded[:], tables[0][:])
         nc.scalar.activation(x_picked[:, 0, :], table0_rounded[:].indirect(offsets[:, 0:cols]), COPY)
-        nc.scalar.copy(warm_weight_values[:].rearrange("p c j -> p (c j)"), tables[2][:, 0:128])
         for l in range(1, 3):
             gather(l, 0, V)
-        quantize(warm_weights[:], warm_weight_scales[:], warm_weight_values[:])
         for half in range(2):
             gather(3, half * HALF, (half + 1) * HALF)
+        quantize(warm_weights[:], warm_weight_scales[:], x_picked[:, 3, 0:HALF].rearrange("p (c j) -> p c j", j=4))
         for c in range(3):
             for pair in range(2):
                 w1_copy(nc.scalar.copy, c, pair)
@@ -142,7 +141,8 @@ def tile_picked_grid_mlp_relu_sub_l_kernel(tc, xT, w1, w2, offs, out):
         for t in range(4):
             quantize_w1(t, 1)
         x_codes.append(keep.tile([P, HALF], U32, name="x_codes1", tag="grouped10", align_bytes=64))
-        quantize(x_codes[1][:], x_scales[:, halves[1]], x_grouped[1][:])
+        for half, a, b in groups[1:]:
+            quantize(x_codes[1][:, a:b], x_scales[:, HALF + a : HALF + b], x_grouped[1][:, a:b, :])
         for g, (half, a, b) in enumerate(groups):
             v = slice(half * HALF + a, half * HALF + b)
             for t in range(4):

@@ -163,18 +163,14 @@ def tile_picked_grid_mlp_relu_sub_l_kernel(tc, xT, w1, w2, offs, out):
         nc.vector.tensor_scalar_max(h_grouped[1][:, 0:64, :], hidden[1][:].rearrange("p t v -> p v t"), 0.0)
         nc.scalar.activation(h_grouped[1][:, 64:HALF, :], hidden[2][:].rearrange("p t v -> p v t"), RELU)
         out_view = out.rearrange("(u p) v -> p u v", u=2)
+        for half, a, b in groups:
+            v = slice(half * HALF + a, half * HALF + b)
+            quantize(h_codes[:, v], h_scales[:, v], h_grouped[half][:, a:b, :])
         for half, v in enumerate(halves):
-            quantize(h_codes[:, v], h_scales[:, v], h_grouped[half][:])
-        acc0 = psum.tile([P, 2, HALF], F32, name="acc0")
-        for u, n in enumerate(halves):
-            product(acc0[:, u, :], w2_codes[:, n], w2_scales[:, n], h_codes[:, halves[0]], h_scales[:, halves[0]])
-        result0 = keep.tile([P, 2, HALF], F32, name="result0")
-        nc.vector.tensor_copy(result0[:], acc0[:])
-        nc.sync.dma_start(out_view[:, :, halves[0]], result0[:])
-        result1 = keep.tile([P, 2, HALF], F32, name="result1")
-        for u, n in enumerate(halves):
-            acc = psum.tile([P, HALF], F32, name=f"acc1{u}")
-            product(acc[:], w2_codes[:, n], w2_scales[:, n], h_codes[:, halves[1]], h_scales[:, halves[1]])
-            copy = nc.scalar.copy if u == 0 else nc.vector.tensor_copy
-            copy(result1[:, u, :], acc[:])
-        nc.sync.dma_start(out_view[:, :, halves[1]], result1[:])
+            result = keep.tile([P, 2, HALF], F32, name=f"result{half}")
+            for u, n in enumerate(halves):
+                acc = psum.tile([P, HALF], F32, name=f"acc{half}{u}")
+                product(acc[:], w2_codes[:, n], w2_scales[:, n], h_codes[:, v], h_scales[:, v])
+                copy = nc.scalar.copy if u == 0 else nc.vector.tensor_copy
+                copy(result[:, u, :], acc[:])
+            nc.sync.dma_start(out_view[:, :, v], result[:])

@@ -29,17 +29,20 @@ def tile_picked_grid_mlp_relu_sub_l_kernel(tc, xT, w1, w2, offs, out):
         offsets = keep.tile([P, D * V // 16], U16, name="offsets")
         x_rows = xT.rearrange("(p l) w -> p l w", l=4)
         tables = []
-        for l in range(4):
+        first_tables = keep.tile([P, 2, T], F32, name="first_tables")
+        nc.sync.dma_start(first_tables[:], x_rows[:, 0:2, :])
+        nc.sync.dma_start(offsets[:], offs)
+        tables += [first_tables[:, 0, :], first_tables[:, 1, :]]
+        for l in range(2, 4):
             table = keep.tile([P, T], F32, name=f"table{l}")
             nc.sync.dma_start(table[:], x_rows[:, l, :])
-            tables.append(table)
-            if l == 0:
-                nc.sync.dma_start(offsets[:], offs)
+            tables.append(table[:])
         w1_rows = w1.rearrange("(p j) i -> p j i", j=4)
         w1_raw = []
-        for c in range(4):
-            raw = keep.tile([P, 4, CHUNK], F32, name=f"w1_raw{c}")
-            nc.sync.dma_start(raw[:], w1_rows[:, :, c * CHUNK : (c + 1) * CHUNK])
+        w1_chunks = [(c * CHUNK, (c + 1) * CHUNK) for c in range(4)]
+        for c, (a, b) in enumerate(w1_chunks):
+            raw = keep.tile([P, 4, b - a], F32, name=f"w1_raw{c}")
+            nc.sync.dma_start(raw[:], w1_rows[:, :, a:b])
             w1_raw.append(raw)
         w2_rows = w2.rearrange("(p t) n -> p t n", t=4)
         w2_raw = []
@@ -49,7 +52,7 @@ def tile_picked_grid_mlp_relu_sub_l_kernel(tc, xT, w1, w2, offs, out):
             nc.sync.dma_start(raw[:], w2_rows[:, :, n])
             w2_raw.append(raw)
 
-        x_picked = keep.tile([P, 4, V], BF16, name="x_picked", align_bytes=64)
+        x_picked = keep.tile([P, 2, 4, HALF], BF16, name="x_picked", align_bytes=64)
         x_grouped = [
             keep.tile([P, HALF, 4], BF16, name=f"x_grouped{half}", tag=f"x_then_w2{half}", align_bytes=64)
             for half in range(2)
@@ -76,8 +79,9 @@ def tile_picked_grid_mlp_relu_sub_l_kernel(tc, xT, w1, w2, offs, out):
             )
 
         def w1_copy(copy, c, pair):
-            m = slice(c % 2 * 32, (c % 2 + 1) * 32)
-            dst = w1_grouped[c // 2][pair][:, :, m, :].rearrange("p t m j -> p m j t")
+            a, b = w1_chunks[c]
+            m = slice(a % 256 // 4, a % 256 // 4 + (b - a) // 4)
+            dst = w1_grouped[a // 256][pair][:, :, m, :].rearrange("p t m j -> p m j t")
             src = w1_raw[c][:].rearrange("p j (m t) -> p m j t", t=4)[:, :, :, 2 * pair : 2 * pair + 2]
             copy(out=dst, in_=src)
 
@@ -89,7 +93,7 @@ def tile_picked_grid_mlp_relu_sub_l_kernel(tc, xT, w1, w2, offs, out):
 
         def gather(l, v0, v1):
             c0, c1 = l * cols + v0 // 16, l * cols + v1 // 16
-            nc.vector.tensor_copy(x_picked[:, l, v0:v1], tables[l][:].indirect(offsets[:, c0:c1]))
+            nc.vector.tensor_copy(x_picked[:, v0 // HALF : v1 // HALF, l, :], tables[l].indirect(offsets[:, c0:c1]))
 
         halves = [slice(half * HALF, (half + 1) * HALF) for half in range(2)]
         groups = [(0, 0, HALF), (1, 0, 64), (1, 64, HALF)]
@@ -117,18 +121,18 @@ def tile_picked_grid_mlp_relu_sub_l_kernel(tc, xT, w1, w2, offs, out):
         nc.scalar.activation(warm_values[:, 0:16, :].rearrange("p c j -> p (c j)"), warm_seed[:], RELU)
         quantize(warm_codes[:], warm_scales[:], warm_values[:])
         table0_rounded = keep.tile([P, T], BF16, name="table0_rounded", align_bytes=64)
-        nc.scalar.copy(table0_rounded[:], tables[0][:])
-        nc.scalar.activation(x_picked[:, 0, :], table0_rounded[:].indirect(offsets[:, 0:cols]), COPY)
+        nc.scalar.copy(table0_rounded[:], tables[0])
+        nc.scalar.activation(x_picked[:, :, 0, :], table0_rounded[:].indirect(offsets[:, 0:cols]), COPY)
         for l in range(1, 3):
             gather(l, 0, V)
         for half in range(2):
             gather(3, half * HALF, (half + 1) * HALF)
-        quantize(warm_weights[:], warm_weight_scales[:], x_picked[:, 3, 0:HALF].rearrange("p (c j) -> p c j", j=4))
+        quantize(warm_weights[:], warm_weight_scales[:], x_picked[:, 0, 3, :].rearrange("p (c j) -> p c j", j=4))
         for c in range(3):
             for pair in range(2):
                 w1_copy(nc.scalar.copy, c, pair)
         for half, v in enumerate(halves):
-            interleave(nc.vector.tensor_copy, x_grouped[half][:], x_picked[:, :, v])
+            interleave(nc.vector.tensor_copy, x_grouped[half][:], x_picked[:, half, :, :])
         x_codes = [keep.tile([P, HALF], U32, name="x_codes0", align_bytes=64)]
         quantize(x_codes[0][:], x_scales[:, halves[0]], x_grouped[0][:])
         warm = psum.tile([32, HALF], F32, name="warm")

@@ -29,14 +29,12 @@ def tile_picked_grid_mlp_relu_sub_l_kernel(tc, xT, w1, w2, offs, out):
         offsets = keep.tile([P, D * V // 16], U16, name="offsets")
         x_rows = xT.rearrange("(p l) w -> p l w", l=4)
         tables = []
-        first_tables = keep.tile([P, 2, T], F32, name="first_tables")
-        nc.sync.dma_start(first_tables[:], x_rows[:, 0:2, :])
-        nc.sync.dma_start(offsets[:], offs)
-        tables += [first_tables[:, 0, :], first_tables[:, 1, :]]
-        for l in range(2, 4):
+        for l in range(4):
             table = keep.tile([P, T], F32, name=f"table{l}")
             nc.sync.dma_start(table[:], x_rows[:, l, :])
             tables.append(table[:])
+            if l == 0:
+                nc.sync.dma_start(offsets[:], offs)
         w1_rows = w1.rearrange("(p j) i -> p j i", j=4)
         w1_raw = []
         w1_chunks = [(c * CHUNK, (c + 1) * CHUNK) for c in range(4)]
@@ -121,9 +119,9 @@ def tile_picked_grid_mlp_relu_sub_l_kernel(tc, xT, w1, w2, offs, out):
         nc.scalar.activation(warm_values[:, 0:16, :].rearrange("p c j -> p (c j)"), warm_seed[:], RELU)
         quantize(warm_codes[:], warm_scales[:], warm_values[:])
         table0_rounded = keep.tile([P, T], BF16, name="table0_rounded", align_bytes=64)
-        nc.scalar.copy(table0_rounded[:], tables[0])
-        nc.scalar.activation(x_picked[:, :, 0, :], table0_rounded[:].indirect(offsets[:, 0:cols]), COPY)
-        for l in range(1, 3):
+        nc.scalar.copy(table0_rounded[:], tables[1])
+        nc.scalar.activation(x_picked[:, :, 1, :], table0_rounded[:].indirect(offsets[:, cols : 2 * cols]), COPY)
+        for l in (0, 2):
             gather(l, 0, V)
         for half in range(2):
             gather(3, half * HALF, (half + 1) * HALF)

@@ -18,6 +18,7 @@ HALF = 128
 
 CHUNK = 128
 WARM_PASSES = 12
+SCALAR_SHARE = 24
 
 
 def tile_picked_grid_mlp_relu_sub_l_kernel(tc, xT, w1, w2, offs, out):
@@ -76,11 +77,11 @@ def tile_picked_grid_mlp_relu_sub_l_kernel(tc, xT, w1, w2, offs, out):
                 in_=planes.rearrange("p t (c i) -> p c t i", i=4),
             )
 
-        def w1_copy(copy, c, pair):
+        def w1_copy(copy, c, pair, lo=0, hi=CHUNK // 4):
             a, b = w1_chunks[c]
-            m = slice(a % 256 // 4, a % 256 // 4 + (b - a) // 4)
+            m = slice(a % 256 // 4 + lo, a % 256 // 4 + hi)
             dst = w1_grouped[a // 256][pair][:, :, m, :].rearrange("p t m j -> p m j t")
-            src = w1_raw[c][:].rearrange("p j (m t) -> p m j t", t=4)[:, :, :, 2 * pair : 2 * pair + 2]
+            src = w1_raw[c][:].rearrange("p j (m t) -> p m j t", t=4)[:, lo:hi, :, 2 * pair : 2 * pair + 2]
             copy(out=dst, in_=src)
 
         def quantize_w1(t, s):
@@ -126,9 +127,9 @@ def tile_picked_grid_mlp_relu_sub_l_kernel(tc, xT, w1, w2, offs, out):
         for half in range(2):
             gather(3, half * HALF, (half + 1) * HALF)
         quantize(warm_weights[:], warm_weight_scales[:], x_picked[:, 0, 3, :].rearrange("p (c j) -> p c j", j=4))
-        for c in range(3):
-            for pair in range(2):
-                w1_copy(nc.scalar.copy, c, pair)
+        for c, pair in ((0, 0), (0, 1), (1, 0), (1, 1), (2, 0)):
+            w1_copy(nc.scalar.copy, c, pair)
+        w1_copy(nc.scalar.copy, 3, 0, 0, SCALAR_SHARE)
         for half, v in enumerate(halves):
             interleave(nc.vector.tensor_copy, x_grouped[half][:], x_picked[:, half, :, :])
         x_codes = [keep.tile([P, HALF], U32, name="x_codes0", align_bytes=64)]
@@ -136,10 +137,13 @@ def tile_picked_grid_mlp_relu_sub_l_kernel(tc, xT, w1, w2, offs, out):
         warm = psum.tile([32, HALF], F32, name="warm")
         for repeat in range(WARM_PASSES):
             product(warm[:], warm_weights[:], warm_weight_scales[:], warm_codes[:], warm_scales[:])
-        for t in range(4):
+        for t in range(2):
             quantize_w1(t, 0)
-        for pair in range(2):
-            w1_copy(nc.vector.tensor_copy, 3, pair)
+        w1_copy(nc.vector.tensor_copy, 2, 1)
+        for t in range(2, 4):
+            quantize_w1(t, 0)
+        w1_copy(nc.vector.tensor_copy, 3, 0, SCALAR_SHARE, CHUNK // 4)
+        w1_copy(nc.vector.tensor_copy, 3, 1)
         for t in range(4):
             quantize_w1(t, 1)
         x_codes.append(keep.tile([P, HALF], U32, name="x_codes1", tag="grouped10", align_bytes=64))

@@ -18,7 +18,7 @@ HALF = 128
 
 CHUNK = 128
 WARM_PASSES = 12
-SCALAR_SHARE = 24
+SCALAR_SHARE = 10
 
 
 def tile_picked_grid_mlp_relu_sub_l_kernel(tc, xT, w1, w2, offs, out):

@@ -17,7 +17,9 @@ COPY = mybir.ActivationFunctionType.Copy
 HALF = 128
 
 CHUNK = 128
-WARM_PASSES = 12
+WARM_PASSES = 2
+WARM_COLUMNS = 512
+TWO_ONES = 0x3F803F80
 SCALAR_SHARE = 10
 
 
@@ -109,15 +111,14 @@ def tile_picked_grid_mlp_relu_sub_l_kernel(tc, xT, w1, w2, offs, out):
                 stop=True,
             )
 
-        warm_values = keep.tile([P, HALF, 4], BF16, name="warm_values", align_bytes=64)
-        warm_codes = keep.tile([P, HALF], U32, name="warm_codes", align_bytes=64)
-        warm_scales = keep.tile([P, HALF], U8, name="warm_scales", align_bytes=64)
+        warm_values = keep.tile([P, WARM_COLUMNS, 4], BF16, name="warm_values", align_bytes=64)
+        warm_codes = keep.tile([P, WARM_COLUMNS], U32, name="warm_codes", align_bytes=64)
+        warm_scales = keep.tile([P, WARM_COLUMNS], U8, name="warm_scales", align_bytes=64)
         warm_weights = keep.tile([P, 32], U32, name="warm_weights", align_bytes=64)
         warm_weight_scales = keep.tile([P, 32], U8, name="warm_weight_scales", align_bytes=64)
-        warm_seed = keep.tile([P, 64], BF16, name="warm_seed")
-        nc.vector.memset(warm_seed[:], 1.0)
-        nc.vector.memset(warm_values[:, 16:, :], 1.0)
-        nc.scalar.activation(warm_values[:, 0:16, :].rearrange("p c j -> p (c j)"), warm_seed[:], RELU)
+        warm_relu = keep.tile([P, 64], BF16, name="warm_relu")
+        nc.vector.memset(warm_values[:].rearrange("p c j -> p (c j)").bitcast(U32), TWO_ONES)
+        nc.scalar.activation(warm_relu[:], warm_values[:, 0:16, :].rearrange("p c j -> p (c j)"), RELU)
         quantize(warm_codes[:], warm_scales[:], warm_values[:])
         table0_rounded = keep.tile([P, T], BF16, name="table0_rounded", align_bytes=64)
         nc.scalar.copy(table0_rounded[:], tables[1])
@@ -134,7 +135,7 @@ def tile_picked_grid_mlp_relu_sub_l_kernel(tc, xT, w1, w2, offs, out):
             interleave(nc.vector.tensor_copy, x_grouped[half][:], x_picked[:, half, :, :])
         x_codes = [keep.tile([P, HALF], U32, name="x_codes0", align_bytes=64)]
         quantize(x_codes[0][:], x_scales[:, halves[0]], x_grouped[0][:])
-        warm = psum.tile([32, HALF], F32, name="warm")
+        warm = psum.tile([32, WARM_COLUMNS], F32, name="warm")
         for repeat in range(WARM_PASSES):
             product(warm[:], warm_weights[:], warm_weight_scales[:], warm_codes[:], warm_scales[:])
         for t in range(2):
@@ -165,18 +166,22 @@ def tile_picked_grid_mlp_relu_sub_l_kernel(tc, xT, w1, w2, offs, out):
         for half in range(2):
             grouped = keep.tile([P, HALF, 4], BF16, name=f"h_grouped{half}", tag=f"w2_then_h{half}", align_bytes=64)
             h_grouped.append(grouped)
-        nc.scalar.activation(h_grouped[0][:], hidden[0][:].rearrange("p t v -> p v t"), RELU)
+        for a, b in ((0, 64), (64, HALF)):
+            nc.scalar.activation(h_grouped[0][:, a:b, :], hidden[0][:, :, a:b].rearrange("p t v -> p v t"), RELU)
         nc.vector.tensor_scalar_max(h_grouped[1][:, 0:64, :], hidden[1][:].rearrange("p t v -> p v t"), 0.0)
         nc.scalar.activation(h_grouped[1][:, 64:HALF, :], hidden[2][:].rearrange("p t v -> p v t"), RELU)
         out_view = out.rearrange("(u p) v -> p u v", u=2)
-        for half, a, b in groups:
-            v = slice(half * HALF + a, half * HALF + b)
-            quantize(h_codes[:, v], h_scales[:, v], h_grouped[half][:, a:b, :])
+        for half in range(2):
+            for a, b in ((0, 64), (64, HALF)):
+                v = slice(half * HALF + a, half * HALF + b)
+                quantize(h_codes[:, v], h_scales[:, v], h_grouped[half][:, a:b, :])
         for half, v in enumerate(halves):
             result = keep.tile([P, 2, HALF], F32, name=f"result{half}")
-            for u, n in enumerate(halves):
-                acc = psum.tile([P, HALF], F32, name=f"acc{half}{u}")
-                product(acc[:], w2_codes[:, n], w2_scales[:, n], h_codes[:, v], h_scales[:, v])
-                copy = nc.scalar.copy if u == 0 else nc.vector.tensor_copy
-                copy(result[:, u, :], acc[:])
+            accs = [psum.tile([P, HALF], F32, name=f"acc{half}{u}") for u in range(2)]
+            for a, b in ((0, 64), (64, HALF)):
+                g = slice(half * HALF + a, half * HALF + b)
+                for u, n in enumerate(halves):
+                    product(accs[u][:, a:b], w2_codes[:, n], w2_scales[:, n], h_codes[:, g], h_scales[:, g])
+            nc.scalar.copy(result[:, 0, :], accs[0][:])
+            nc.vector.tensor_copy(result[:, 1, :], accs[1][:])
             nc.sync.dma_start(out_view[:, :, v], result[:])

@@ -34,7 +34,8 @@ def tile_picked_grid_mlp_relu_sub_l_kernel(tc, xT, w1, w2, offs, out):
         tables = []
         for l in range(4):
             table = keep.tile([P, T], F32, name=f"table{l}")
-            nc.sync.dma_start(table[:], x_rows[:, l, :])
+            queue = nc.scalar if l == 1 else nc.sync
+            queue.dma_start(table[:], x_rows[:, l, :])
             tables.append(table[:])
             if l == 0:
                 nc.sync.dma_start(offsets[:], offs)
@@ -127,7 +128,7 @@ def tile_picked_grid_mlp_relu_sub_l_kernel(tc, xT, w1, w2, offs, out):
             gather(l, 0, V)
         for half in range(2):
             gather(3, half * HALF, (half + 1) * HALF)
-        quantize(warm_weights[:], warm_weight_scales[:], x_picked[:, 0, 3, :].rearrange("p (c j) -> p c j", j=4))
+        quantize(warm_weights[:], warm_weight_scales[:], x_picked[:, 1, 3, :].rearrange("p (c j) -> p c j", j=4))
         for c, pair in ((0, 0), (0, 1), (1, 0), (1, 1), (2, 0)):
             w1_copy(nc.scalar.copy, c, pair)
         w1_copy(nc.scalar.copy, 3, 0, 0, SCALAR_SHARE)

@@ -185,4 +185,8 @@ def tile_picked_grid_mlp_relu_sub_l_kernel(tc, xT, w1, w2, offs, out):
                     product(accs[u][:, a:b], w2_codes[:, n], w2_scales[:, n], h_codes[:, g], h_scales[:, g])
             nc.scalar.copy(result[:, 0, :], accs[0][:])
             nc.vector.tensor_copy(result[:, 1, :], accs[1][:])
-            nc.sync.dma_start(out_view[:, :, v], result[:])
+            if half == 0:
+                nc.sync.dma_start(out_view[:, :, v], result[:])
+            else:
+                nc.scalar.dma_start(out_view[:, 0, v], result[:, 0, :])
+                nc.sync.dma_start(out_view[:, 1, v], result[:, 1, :])

@@ -34,8 +34,12 @@ def tile_picked_grid_mlp_relu_sub_l_kernel(tc, xT, w1, w2, offs, out):
         tables = []
         for l in range(4):
             table = keep.tile([P, T], F32, name=f"table{l}")
-            queue = nc.scalar if l == 1 else nc.sync
-            queue.dma_start(table[:], x_rows[:, l, :])
+            if l < 2:
+                queue = nc.scalar if l == 1 else nc.sync
+                queue.dma_start(table[:], x_rows[:, l, :])
+            else:
+                nc.sync.dma_start(table[:, 0 : T // 2], x_rows[:, l, 0 : T // 2])
+                nc.scalar.dma_start(table[:, T // 2 : T], x_rows[:, l, T // 2 : T])
             tables.append(table[:])
             if l == 0:
                 nc.sync.dma_start(offsets[:], offs)

@@ -17,9 +17,6 @@ COPY = mybir.ActivationFunctionType.Copy
 HALF = 128
 
 CHUNK = 128
-WARM_PASSES = 2
-WARM_COLUMNS = 512
-TWO_ONES = 0x3F803F80
 SCALAR_SHARE = 10
 
 
@@ -116,15 +113,6 @@ def tile_picked_grid_mlp_relu_sub_l_kernel(tc, xT, w1, w2, offs, out):
                 stop=True,
             )
 
-        warm_values = keep.tile([P, WARM_COLUMNS, 4], BF16, name="warm_values", align_bytes=64)
-        warm_codes = keep.tile([P, WARM_COLUMNS], U32, name="warm_codes", align_bytes=64)
-        warm_scales = keep.tile([P, WARM_COLUMNS], U8, name="warm_scales", align_bytes=64)
-        warm_weights = keep.tile([P, 32], U32, name="warm_weights", align_bytes=64)
-        warm_weight_scales = keep.tile([P, 32], U8, name="warm_weight_scales", align_bytes=64)
-        warm_relu = keep.tile([P, 64], BF16, name="warm_relu")
-        nc.vector.memset(warm_values[:].rearrange("p c j -> p (c j)").bitcast(U32), TWO_ONES)
-        nc.scalar.activation(warm_relu[:], warm_values[:, 0:16, :].rearrange("p c j -> p (c j)"), RELU)
-        quantize(warm_codes[:], warm_scales[:], warm_values[:])
         table0_rounded = keep.tile([P, T], BF16, name="table0_rounded", align_bytes=64)
         nc.scalar.copy(table0_rounded[:], tables[1])
         nc.scalar.activation(x_picked[:, :, 1, :], table0_rounded[:].indirect(offsets[:, cols : 2 * cols]), COPY)
@@ -132,7 +120,6 @@ def tile_picked_grid_mlp_relu_sub_l_kernel(tc, xT, w1, w2, offs, out):
             gather(l, 0, V)
         for half in range(2):
             gather(3, half * HALF, (half + 1) * HALF)
-        quantize(warm_weights[:], warm_weight_scales[:], x_picked[:, 1, 3, :].rearrange("p (c j) -> p c j", j=4))
         for c, pair in ((0, 0), (0, 1), (1, 0), (1, 1), (2, 0)):
             w1_copy(nc.scalar.copy, c, pair)
         w1_copy(nc.scalar.copy, 3, 0, 0, SCALAR_SHARE)
@@ -140,9 +127,6 @@ def tile_picked_grid_mlp_relu_sub_l_kernel(tc, xT, w1, w2, offs, out):
             interleave(nc.vector.tensor_copy, x_grouped[half][:], x_picked[:, half, :, :])
         x_codes = [keep.tile([P, HALF], U32, name="x_codes0", align_bytes=64)]
         quantize(x_codes[0][:], x_scales[:, halves[0]], x_grouped[0][:])
-        warm = psum.tile([32, WARM_COLUMNS], F32, name="warm")
-        for repeat in range(WARM_PASSES):
-            product(warm[:], warm_weights[:], warm_weight_scales[:], warm_codes[:], warm_scales[:])
         for t in range(2):
             quantize_w1(t, 0)
         w1_copy(nc.vector.tensor_copy, 2, 1)

@@ -14,9 +14,15 @@ U8 = mybir.dt.uint8
 FP8X4 = mybir.dt.float8_e4m3fn_x4
 RELU = mybir.ActivationFunctionType.Relu
 COPY = mybir.ActivationFunctionType.Copy
-HALF = 128
 
-CHUNK = 128
+PACK = 4
+ALIGN = 64
+HALF = V // 2
+BLOCK = N // 2
+CHUNK = H // 4
+CHUNK_COLUMNS = CHUNK // PACK
+PART = 2 * CHUNK_COLUMNS
+LIST_COLUMNS = V // 16
 SCALAR_SHARE = 10
 
 
@@ -26,81 +32,79 @@ def tile_picked_grid_mlp_relu_sub_l_kernel(tc, xT, w1, w2, offs, out):
         keep = ctx.enter_context(tc.tile_pool(name="keep", bufs=1))
         psum = ctx.enter_context(tc.psum_pool(name="psum", bufs=1))
 
-        offsets = keep.tile([P, D * V // 16], U16, name="offsets")
-        x_rows = xT.rearrange("(p l) w -> p l w", l=4)
+        offsets = keep.tile([P, D * LIST_COLUMNS], U16, name="offsets")
+        x_rows = xT.rearrange("(p l) w -> p l w", l=D)
         tables = []
-        for l in range(4):
-            table = keep.tile([P, T], F32, name=f"table{l}")
-            if l < 2:
-                queue = nc.scalar if l == 1 else nc.sync
-                queue.dma_start(table[:], x_rows[:, l, :])
+        for level in range(D):
+            table = keep.tile([P, T], F32, name=f"table{level}")
+            if level < 2:
+                queue = nc.scalar if level == 1 else nc.sync
+                queue.dma_start(table[:], x_rows[:, level, :])
             else:
-                nc.sync.dma_start(table[:, 0 : T // 2], x_rows[:, l, 0 : T // 2])
-                nc.scalar.dma_start(table[:, T // 2 : T], x_rows[:, l, T // 2 : T])
+                nc.sync.dma_start(table[:, 0 : T // 2], x_rows[:, level, 0 : T // 2])
+                nc.scalar.dma_start(table[:, T // 2 : T], x_rows[:, level, T // 2 : T])
             tables.append(table[:])
-            if l == 0:
+            if level == 0:
                 nc.sync.dma_start(offsets[:], offs)
-        w1_rows = w1.rearrange("(p j) i -> p j i", j=4)
+        w1_rows = w1.rearrange("(p j) i -> p j i", j=PACK)
         w1_raw = []
-        w1_chunks = [(c * CHUNK, (c + 1) * CHUNK) for c in range(4)]
-        for c, (a, b) in enumerate(w1_chunks):
-            raw = keep.tile([P, 4, b - a], F32, name=f"w1_raw{c}")
-            nc.sync.dma_start(raw[:], w1_rows[:, :, a:b])
+        for chunk in range(H // CHUNK):
+            raw = keep.tile([P, PACK, CHUNK], F32, name=f"w1_raw{chunk}")
+            nc.sync.dma_start(raw[:], w1_rows[:, :, chunk * CHUNK : (chunk + 1) * CHUNK])
             w1_raw.append(raw)
-        w2_rows = w2.rearrange("(p t) n -> p t n", t=4)
+        blocks = [slice(u * BLOCK, (u + 1) * BLOCK) for u in range(2)]
+        w2_rows = w2.rearrange("(p j) n -> p j n", j=PACK)
         w2_raw = []
-        for u in range(2):
-            n = slice(u * 128, (u + 1) * 128)
-            raw = keep.tile([P, 4, 128], F32, name=f"w2_raw{u}", tag=f"w2_then_h{u}", align_bytes=64)
-            nc.sync.dma_start(raw[:], w2_rows[:, :, n])
+        for u, rows in enumerate(blocks):
+            raw = keep.tile([P, PACK, BLOCK], F32, name=f"w2_raw{u}", tag=f"w2_then_h{u}", align_bytes=ALIGN)
+            nc.sync.dma_start(raw[:], w2_rows[:, :, rows])
             w2_raw.append(raw)
 
-        x_picked = keep.tile([P, 2, 4, HALF], BF16, name="x_picked", align_bytes=64)
+        x_picked = keep.tile([P, 2, D, HALF], BF16, name="x_picked", align_bytes=ALIGN)
         x_grouped = [
-            keep.tile([P, HALF, 4], BF16, name=f"x_grouped{half}", tag=f"x_then_w2{half}", align_bytes=64)
+            keep.tile([P, HALF, PACK], BF16, name=f"x_grouped{half}", tag=f"x_then_w2{half}", align_bytes=ALIGN)
             for half in range(2)
         ]
-        x_scales = keep.tile([P, V], U8, name="x_scales", align_bytes=64)
+        x_scales = keep.tile([P, V], U8, name="x_scales", align_bytes=ALIGN)
         w1_grouped = [
-            [keep.tile([P, 2, 64, 4], BF16, name=f"w1_grouped{s}{pair}", tag=f"grouped{s}{pair}", align_bytes=64) for pair in range(2)]
-            for s in range(2)
+            [
+                keep.tile([P, 2, PART, PACK], BF16, name=f"w1_grouped{part}{pair}", tag=f"grouped{part}{pair}", align_bytes=ALIGN)
+                for pair in range(2)
+            ]
+            for part in range(2)
         ]
-        w1_codes = [keep.tile([P, 128], U32, name=f"w1_codes{t}", align_bytes=64) for t in range(4)]
-        w1_scales = [keep.tile([P, 128], U8, name=f"w1_scales{t}", align_bytes=64) for t in range(4)]
-        w2_codes = keep.tile([P, N], U32, name="w2_codes", align_bytes=64)
-        w2_scales = keep.tile([P, N], U8, name="w2_scales", align_bytes=64)
-        h_codes = keep.tile([P, V], U32, name="h_codes", align_bytes=64)
-        h_scales = keep.tile([P, V], U8, name="h_scales", align_bytes=64)
+        w1_codes = [keep.tile([P, P], U32, name=f"w1_codes{t}", align_bytes=ALIGN) for t in range(PACK)]
+        w1_scales = [keep.tile([P, P], U8, name=f"w1_scales{t}", align_bytes=ALIGN) for t in range(PACK)]
+        w2_codes = keep.tile([P, N], U32, name="w2_codes", align_bytes=ALIGN)
+        w2_scales = keep.tile([P, N], U8, name="w2_scales", align_bytes=ALIGN)
+        h_codes = keep.tile([P, V], U32, name="h_codes", align_bytes=ALIGN)
+        h_scales = keep.tile([P, V], U8, name="h_scales", align_bytes=ALIGN)
 
         def quantize(codes, scales, grouped):
             nc.vector.quantize_mx(out=codes.bitcast(FP8X4), scales=scales, in_=grouped.rearrange("p c j -> p (c j)"))
 
         def interleave(copy, grouped, planes):
             copy(
-                out=grouped.rearrange("p (c i) t -> p c t i", i=4),
-                in_=planes.rearrange("p t (c i) -> p c t i", i=4),
+                out=grouped.rearrange("p (c i) j -> p c j i", i=4),
+                in_=planes.rearrange("p j (c i) -> p c j i", i=4),
             )
 
-        def w1_copy(copy, c, pair, lo=0, hi=CHUNK // 4):
-            a, b = w1_chunks[c]
-            m = slice(a % 256 // 4 + lo, a % 256 // 4 + hi)
-            dst = w1_grouped[a // 256][pair][:, :, m, :].rearrange("p t m j -> p m j t")
-            src = w1_raw[c][:].rearrange("p j (m t) -> p m j t", t=4)[:, lo:hi, :, 2 * pair : 2 * pair + 2]
+        def round_w1(copy, chunk, pair, lo=0, hi=CHUNK_COLUMNS):
+            start = chunk % 2 * CHUNK_COLUMNS
+            dst = w1_grouped[chunk // 2][pair][:, :, start + lo : start + hi, :].rearrange("p t m j -> p m j t")
+            src = w1_raw[chunk][:].rearrange("p j (m t) -> p m j t", t=PACK)[:, lo:hi, :, 2 * pair : 2 * pair + 2]
             copy(out=dst, in_=src)
 
-        def quantize_w1(t, s):
-            m = slice(s * 64, (s + 1) * 64)
-            quantize(w1_codes[t][:, m], w1_scales[t][:, m], w1_grouped[s][t // 2][:, t % 2, :, :])
+        def quantize_w1(t, part):
+            m = slice(part * PART, (part + 1) * PART)
+            quantize(w1_codes[t][:, m], w1_scales[t][:, m], w1_grouped[part][t // 2][:, t % 2, :, :])
 
-        cols = V // 16
+        def level_offsets(level, v0, v1):
+            return offsets[:, level * LIST_COLUMNS + v0 // 16 : level * LIST_COLUMNS + v1 // 16]
 
-        def gather(l, v0, v1):
-            c0, c1 = l * cols + v0 // 16, l * cols + v1 // 16
-            nc.vector.tensor_copy(x_picked[:, v0 // HALF : v1 // HALF, l, :], tables[l].indirect(offsets[:, c0:c1]))
-
-        halves = [slice(half * HALF, (half + 1) * HALF) for half in range(2)]
-        groups = [(0, 0, HALF), (1, 0, 64), (1, 64, HALF)]
-        hidden = [psum.tile([P, 4, b - a], F32, name=f"hidden{half}_{a}") for half, a, b in groups]
+        def gather(level, v0, v1):
+            picked = x_picked[:, v0 // HALF : v1 // HALF, level, :]
+            nc.vector.tensor_copy(picked, tables[level].indirect(level_offsets(level, v0, v1)))
 
         def product(acc, codes, scales, moving, moving_scales):
             nc.tensor.matmul_mx(
@@ -113,64 +117,74 @@ def tile_picked_grid_mlp_relu_sub_l_kernel(tc, xT, w1, w2, offs, out):
                 stop=True,
             )
 
-        table0_rounded = keep.tile([P, T], BF16, name="table0_rounded", align_bytes=64)
-        nc.scalar.copy(table0_rounded[:], tables[1])
-        nc.scalar.activation(x_picked[:, :, 1, :], table0_rounded[:].indirect(offsets[:, cols : 2 * cols]), COPY)
-        for l in (0, 2):
-            gather(l, 0, V)
+        halves = [slice(half * HALF, (half + 1) * HALF) for half in range(2)]
+        first = psum.tile([P, PACK, HALF], F32, name="hidden0")
+        second = [psum.tile([P, 2, HALF], F32, name=f"hidden1{pair}") for pair in range(2)]
+        hidden = [[first[:, t, :] for t in range(PACK)], [second[t // 2][:, t % 2, :] for t in range(PACK)]]
+
+        zero = keep.tile([P, 1], F32, name="zero")
+        nc.vector.memset(zero[:], 0.0)
+        warm = keep.tile([P, 16], F32, name="warm")
+        nc.scalar.activation(warm[:], zero[:].to_broadcast([P, 16]), RELU)
+
+        table1_rounded = keep.tile([P, T], BF16, name="table1_rounded", align_bytes=ALIGN)
+        nc.scalar.copy(table1_rounded[:], tables[1])
+        nc.scalar.activation(x_picked[:, :, 1, :], table1_rounded[:].indirect(level_offsets(1, 0, V)), COPY)
+        for level in (0, 2):
+            gather(level, 0, V)
         for half in range(2):
             gather(3, half * HALF, (half + 1) * HALF)
-        for c, pair in ((0, 0), (0, 1), (1, 0), (1, 1), (2, 0)):
-            w1_copy(nc.scalar.copy, c, pair)
-        w1_copy(nc.scalar.copy, 3, 0, 0, SCALAR_SHARE)
-        for half, v in enumerate(halves):
+
+        for chunk in range(2):
+            for pair in range(2):
+                round_w1(nc.scalar.copy, chunk, pair)
+        round_w1(nc.scalar.copy, 2, 0)
+        round_w1(nc.scalar.copy, 3, 0, 0, SCALAR_SHARE)
+        for half in range(2):
             interleave(nc.vector.tensor_copy, x_grouped[half][:], x_picked[:, half, :, :])
-        x_codes = [keep.tile([P, HALF], U32, name="x_codes0", align_bytes=64)]
+        x_codes = [keep.tile([P, HALF], U32, name="x_codes0", align_bytes=ALIGN)]
         quantize(x_codes[0][:], x_scales[:, halves[0]], x_grouped[0][:])
         for t in range(2):
             quantize_w1(t, 0)
-        w1_copy(nc.vector.tensor_copy, 2, 1)
-        for t in range(2, 4):
+        round_w1(nc.vector.tensor_copy, 2, 1)
+        for t in range(2, PACK):
             quantize_w1(t, 0)
-        w1_copy(nc.vector.tensor_copy, 3, 0, SCALAR_SHARE, CHUNK // 4)
-        w1_copy(nc.vector.tensor_copy, 3, 1)
-        for t in range(4):
+        round_w1(nc.vector.tensor_copy, 3, 0, SCALAR_SHARE, CHUNK_COLUMNS)
+        round_w1(nc.vector.tensor_copy, 3, 1)
+        for t in range(PACK):
             quantize_w1(t, 1)
-        x_codes.append(keep.tile([P, HALF], U32, name="x_codes1", tag="grouped10", align_bytes=64))
-        for half, a, b in groups[1:]:
-            quantize(x_codes[1][:, a:b], x_scales[:, HALF + a : HALF + b], x_grouped[1][:, a:b, :])
-        for g, (half, a, b) in enumerate(groups):
-            v = slice(half * HALF + a, half * HALF + b)
-            for t in range(4):
-                product(hidden[g][:, t, :], w1_codes[t][:], w1_scales[t][:], x_codes[half][:, a:b], x_scales[:, v])
+        x_codes.append(keep.tile([P, HALF], U32, name="x_codes1", tag="grouped10", align_bytes=ALIGN))
+        quantize(x_codes[1][:], x_scales[:, halves[1]], x_grouped[1][:])
+
+        for half, v in enumerate(halves):
+            for t in range(PACK):
+                product(hidden[half][t], w1_codes[t][:], w1_scales[t][:], x_codes[half][:], x_scales[:, v])
+
         w2_grouped = [
-            keep.tile([P, 128, 4], BF16, name="w2_grouped0", align_bytes=64),
-            keep.tile([P, 128, 4], BF16, name="w2_grouped1", tag="x_then_w21", align_bytes=64),
+            keep.tile([P, BLOCK, PACK], BF16, name="w2_grouped0", align_bytes=ALIGN),
+            keep.tile([P, BLOCK, PACK], BF16, name="w2_grouped1", tag="x_then_w21", align_bytes=ALIGN),
         ]
         interleave(nc.scalar.copy, w2_grouped[0][:], w2_raw[0][:])
         interleave(nc.vector.tensor_copy, w2_grouped[1][:], w2_raw[1][:])
-        for u, n in enumerate(halves):
-            quantize(w2_codes[:, n], w2_scales[:, n], w2_grouped[u][:])
-        h_grouped = []
-        for half in range(2):
-            grouped = keep.tile([P, HALF, 4], BF16, name=f"h_grouped{half}", tag=f"w2_then_h{half}", align_bytes=64)
-            h_grouped.append(grouped)
-        for a, b in ((0, 64), (64, HALF)):
-            nc.scalar.activation(h_grouped[0][:, a:b, :], hidden[0][:, :, a:b].rearrange("p t v -> p v t"), RELU)
-        nc.vector.tensor_scalar_max(h_grouped[1][:, 0:64, :], hidden[1][:].rearrange("p t v -> p v t"), 0.0)
-        nc.scalar.activation(h_grouped[1][:, 64:HALF, :], hidden[2][:].rearrange("p t v -> p v t"), RELU)
+        for u, rows in enumerate(blocks):
+            quantize(w2_codes[:, rows], w2_scales[:, rows], w2_grouped[u][:])
+
+        h_grouped = [
+            keep.tile([P, HALF, PACK], BF16, name=f"h_grouped{half}", tag=f"w2_then_h{half}", align_bytes=ALIGN)
+            for half in range(2)
+        ]
+        nc.scalar.activation(h_grouped[0][:], first[:].rearrange("p t v -> p v t"), RELU)
+        nc.scalar.activation(h_grouped[1][:, :, 2:4], second[1][:].rearrange("p t v -> p v t"), RELU)
+        nc.vector.tensor_scalar_max(h_grouped[1][:, :, 0:2], second[0][:].rearrange("p t v -> p v t"), zero[:])
+        for half, v in enumerate(halves):
+            quantize(h_codes[:, v], h_scales[:, v], h_grouped[half][:])
+
         out_view = out.rearrange("(u p) v -> p u v", u=2)
-        for half in range(2):
-            for a, b in ((0, 64), (64, HALF)):
-                v = slice(half * HALF + a, half * HALF + b)
-                quantize(h_codes[:, v], h_scales[:, v], h_grouped[half][:, a:b, :])
         for half, v in enumerate(halves):
             result = keep.tile([P, 2, HALF], F32, name=f"result{half}")
             accs = [psum.tile([P, HALF], F32, name=f"acc{half}{u}") for u in range(2)]
-            for a, b in ((0, 64), (64, HALF)):
-                g = slice(half * HALF + a, half * HALF + b)
-                for u, n in enumerate(halves):
-                    product(accs[u][:, a:b], w2_codes[:, n], w2_scales[:, n], h_codes[:, g], h_scales[:, g])
+            for u, rows in enumerate(blocks):
+                product(accs[u][:], w2_codes[:, rows], w2_scales[:, rows], h_codes[:, v], h_scales[:, v])
             nc.scalar.copy(result[:, 0, :], accs[0][:])
             nc.vector.tensor_copy(result[:, 1, :], accs[1][:])
             if half == 0:

@@ -60,7 +60,7 @@ def tile_picked_grid_mlp_relu_sub_l_kernel(tc, xT, w1, w2, offs, out):
             nc.sync.dma_start(raw[:], w2_rows[:, :, rows])
             w2_raw.append(raw)
 
-        x_picked = keep.tile([P, 2, D, HALF], BF16, name="x_picked", align_bytes=ALIGN)
+        x_picked = keep.tile([P, D, V], BF16, name="x_picked", align_bytes=ALIGN)
         x_grouped = [
             keep.tile([P, HALF, PACK], BF16, name=f"x_grouped{half}", tag=f"x_then_w2{half}", align_bytes=ALIGN)
             for half in range(2)
@@ -103,7 +103,7 @@ def tile_picked_grid_mlp_relu_sub_l_kernel(tc, xT, w1, w2, offs, out):
             return offsets[:, level * LIST_COLUMNS + v0 // 16 : level * LIST_COLUMNS + v1 // 16]
 
         def gather(level, v0, v1):
-            picked = x_picked[:, v0 // HALF : v1 // HALF, level, :]
+            picked = x_picked[:, level, v0:v1]
             nc.vector.tensor_copy(picked, tables[level].indirect(level_offsets(level, v0, v1)))
 
         def product(acc, codes, scales, moving, moving_scales):
@@ -127,13 +127,11 @@ def tile_picked_grid_mlp_relu_sub_l_kernel(tc, xT, w1, w2, offs, out):
         warm = keep.tile([P, 16], F32, name="warm")
         nc.scalar.activation(warm[:], zero[:].to_broadcast([P, 16]), RELU)
 
-        table1_rounded = keep.tile([P, T], BF16, name="table1_rounded", align_bytes=ALIGN)
-        nc.scalar.copy(table1_rounded[:], tables[1])
-        nc.scalar.activation(x_picked[:, :, 1, :], table1_rounded[:].indirect(level_offsets(1, 0, V)), COPY)
+        nc.scalar.activation(x_picked[:, 1, :], tables[1].indirect(level_offsets(1, 0, V)), COPY)
+        nc.scalar.activation(x_picked[:, 3, HALF:V], tables[3].indirect(level_offsets(3, HALF, V)), COPY)
         for level in (0, 2):
             gather(level, 0, V)
-        for half in range(2):
-            gather(3, half * HALF, (half + 1) * HALF)
+        gather(3, 0, HALF)
 
         for chunk in range(2):
             for pair in range(2):
@@ -141,7 +139,7 @@ def tile_picked_grid_mlp_relu_sub_l_kernel(tc, xT, w1, w2, offs, out):
         round_w1(nc.scalar.copy, 2, 0)
         round_w1(nc.scalar.copy, 3, 0, 0, SCALAR_SHARE)
         for half in range(2):
-            interleave(nc.vector.tensor_copy, x_grouped[half][:], x_picked[:, half, :, :])
+            interleave(nc.vector.tensor_copy, x_grouped[half][:], x_picked[:, :, halves[half]])
         x_codes = [keep.tile([P, HALF], U32, name="x_codes0", align_bytes=ALIGN)]
         quantize(x_codes[0][:], x_scales[:, halves[0]], x_grouped[0][:])
         for t in range(2):

@@ -23,7 +23,6 @@ CHUNK = H // 4
 CHUNK_COLUMNS = CHUNK // PACK
 PART = 2 * CHUNK_COLUMNS
 LIST_COLUMNS = V // 16
-SCALAR_SHARE = 10
 
 
 def tile_picked_grid_mlp_relu_sub_l_kernel(tc, xT, w1, w2, offs, out):
@@ -49,7 +48,7 @@ def tile_picked_grid_mlp_relu_sub_l_kernel(tc, xT, w1, w2, offs, out):
         w1_rows = w1.rearrange("(p j) i -> p j i", j=PACK)
         w1_raw = []
         for chunk in range(H // CHUNK):
-            raw = keep.tile([P, PACK, CHUNK], F32, name=f"w1_raw{chunk}")
+            raw = keep.tile([P, PACK, CHUNK], F32, name=f"w1_raw{chunk}", tag=f"w1_raw{chunk}", align_bytes=ALIGN)
             nc.sync.dma_start(raw[:], w1_rows[:, :, chunk * CHUNK : (chunk + 1) * CHUNK])
             w1_raw.append(raw)
         blocks = [slice(u * BLOCK, (u + 1) * BLOCK) for u in range(2)]
@@ -66,13 +65,7 @@ def tile_picked_grid_mlp_relu_sub_l_kernel(tc, xT, w1, w2, offs, out):
             for half in range(2)
         ]
         x_scales = keep.tile([P, V], U8, name="x_scales", align_bytes=ALIGN)
-        w1_grouped = [
-            [
-                keep.tile([P, 2, PART, PACK], BF16, name=f"w1_grouped{part}{pair}", tag=f"grouped{part}{pair}", align_bytes=ALIGN)
-                for pair in range(2)
-            ]
-            for part in range(2)
-        ]
+        w1_grouped = [keep.tile([P, 2, P, PACK], BF16, name=f"w1_grouped{pair}", align_bytes=ALIGN) for pair in range(2)]
         w1_codes = [keep.tile([P, P], U32, name=f"w1_codes{t}", align_bytes=ALIGN) for t in range(PACK)]
         w1_scales = [keep.tile([P, P], U8, name=f"w1_scales{t}", align_bytes=ALIGN) for t in range(PACK)]
         w2_codes = keep.tile([P, N], U32, name="w2_codes", align_bytes=ALIGN)
@@ -89,15 +82,14 @@ def tile_picked_grid_mlp_relu_sub_l_kernel(tc, xT, w1, w2, offs, out):
                 in_=planes.rearrange("p j (c i) -> p c j i", i=4),
             )
 
-        def round_w1(copy, chunk, pair, lo=0, hi=CHUNK_COLUMNS):
-            start = chunk % 2 * CHUNK_COLUMNS
-            dst = w1_grouped[chunk // 2][pair][:, :, start + lo : start + hi, :].rearrange("p t m j -> p m j t")
-            src = w1_raw[chunk][:].rearrange("p j (m t) -> p m j t", t=PACK)[:, lo:hi, :, 2 * pair : 2 * pair + 2]
+        def round_w1(copy, chunk, pair):
+            start = chunk * CHUNK_COLUMNS
+            dst = w1_grouped[pair][:, :, start : start + CHUNK_COLUMNS, :].rearrange("p t m j -> p m j t")
+            src = w1_raw[chunk][:].rearrange("p j (m t) -> p m j t", t=PACK)[:, :, :, 2 * pair : 2 * pair + 2]
             copy(out=dst, in_=src)
 
-        def quantize_w1(t, part):
-            m = slice(part * PART, (part + 1) * PART)
-            quantize(w1_codes[t][:, m], w1_scales[t][:, m], w1_grouped[part][t // 2][:, t % 2, :, :])
+        def quantize_w1(t, m):
+            quantize(w1_codes[t][:, m], w1_scales[t][:, m], w1_grouped[t // 2][:, t % 2, m, :])
 
         def level_offsets(level, v0, v1):
             return offsets[:, level * LIST_COLUMNS + v0 // 16 : level * LIST_COLUMNS + v1 // 16]
@@ -128,30 +120,30 @@ def tile_picked_grid_mlp_relu_sub_l_kernel(tc, xT, w1, w2, offs, out):
         nc.scalar.activation(warm[:], zero[:].to_broadcast([P, 16]), RELU)
 
         nc.scalar.activation(x_picked[:, 1, :], tables[1].indirect(level_offsets(1, 0, V)), COPY)
+        nc.scalar.activation(x_picked[:, 2, :], tables[2].indirect(level_offsets(2, 0, V)), COPY)
         nc.scalar.activation(x_picked[:, 3, HALF:V], tables[3].indirect(level_offsets(3, HALF, V)), COPY)
-        for level in (0, 2):
-            gather(level, 0, V)
+        gather(0, 0, V)
         gather(3, 0, HALF)
 
-        for chunk in range(2):
-            for pair in range(2):
-                round_w1(nc.scalar.copy, chunk, pair)
-        round_w1(nc.scalar.copy, 2, 0)
-        round_w1(nc.scalar.copy, 3, 0, 0, SCALAR_SHARE)
+        round_w1(nc.scalar.copy, 0, 0)
+        round_w1(nc.scalar.copy, 0, 1)
+        round_w1(nc.scalar.copy, 1, 0)
+        round_w1(nc.scalar.copy, 3, 1)
         for half in range(2):
             interleave(nc.vector.tensor_copy, x_grouped[half][:], x_picked[:, :, halves[half]])
         x_codes = [keep.tile([P, HALF], U32, name="x_codes0", align_bytes=ALIGN)]
         quantize(x_codes[0][:], x_scales[:, halves[0]], x_grouped[0][:])
-        for t in range(2):
-            quantize_w1(t, 0)
+        round_w1(nc.vector.tensor_copy, 1, 1)
+        round_w1(nc.vector.tensor_copy, 2, 0)
         round_w1(nc.vector.tensor_copy, 2, 1)
+        for t in range(2):
+            quantize_w1(t, slice(0, PART))
+        round_w1(nc.vector.tensor_copy, 3, 0)
+        for t in range(2):
+            quantize_w1(t, slice(PART, P))
         for t in range(2, PACK):
-            quantize_w1(t, 0)
-        round_w1(nc.vector.tensor_copy, 3, 0, SCALAR_SHARE, CHUNK_COLUMNS)
-        round_w1(nc.vector.tensor_copy, 3, 1)
-        for t in range(PACK):
-            quantize_w1(t, 1)
-        x_codes.append(keep.tile([P, HALF], U32, name="x_codes1", tag="grouped10", align_bytes=ALIGN))
+            quantize_w1(t, slice(0, P))
+        x_codes.append(keep.tile([P, HALF], U32, name="x_codes1", tag="w1_raw3", align_bytes=ALIGN))
         quantize(x_codes[1][:], x_scales[:, halves[1]], x_grouped[1][:])
 
         for half, v in enumerate(halves):

@@ -120,14 +120,15 @@ def tile_picked_grid_mlp_relu_sub_l_kernel(tc, xT, w1, w2, offs, out):
         nc.scalar.activation(warm[:], zero[:].to_broadcast([P, 16]), RELU)
 
         nc.scalar.activation(x_picked[:, 1, :], tables[1].indirect(level_offsets(1, 0, V)), COPY)
-        nc.scalar.activation(x_picked[:, 2, :], tables[2].indirect(level_offsets(2, 0, V)), COPY)
         nc.scalar.activation(x_picked[:, 3, HALF:V], tables[3].indirect(level_offsets(3, HALF, V)), COPY)
-        gather(0, 0, V)
+        for level in (0, 2):
+            gather(level, 0, V)
         gather(3, 0, HALF)
 
         round_w1(nc.scalar.copy, 0, 0)
         round_w1(nc.scalar.copy, 0, 1)
         round_w1(nc.scalar.copy, 1, 0)
+        round_w1(nc.scalar.copy, 2, 1)
         round_w1(nc.scalar.copy, 3, 1)
         for half in range(2):
             interleave(nc.vector.tensor_copy, x_grouped[half][:], x_picked[:, :, halves[half]])
@@ -135,7 +136,6 @@ def tile_picked_grid_mlp_relu_sub_l_kernel(tc, xT, w1, w2, offs, out):
         quantize(x_codes[0][:], x_scales[:, halves[0]], x_grouped[0][:])
         round_w1(nc.vector.tensor_copy, 1, 1)
         round_w1(nc.vector.tensor_copy, 2, 0)
-        round_w1(nc.vector.tensor_copy, 2, 1)
         for t in range(2):
             quantize_w1(t, slice(0, PART))
         round_w1(nc.vector.tensor_copy, 3, 0)

@@ -17,6 +17,7 @@ COPY = mybir.ActivationFunctionType.Copy
 
 PACK = 4
 ALIGN = 64
+ROW_ALIGN = 256
 HALF = V // 2
 BLOCK = N // 2
 CHUNK = H // 4
@@ -31,11 +32,11 @@ def tile_picked_grid_mlp_relu_sub_l_kernel(tc, xT, w1, w2, offs, out):
         keep = ctx.enter_context(tc.tile_pool(name="keep", bufs=1))
         psum = ctx.enter_context(tc.psum_pool(name="psum", bufs=1))
 
-        offsets = keep.tile([P, D * LIST_COLUMNS], U16, name="offsets")
+        offsets = keep.tile([P, D * LIST_COLUMNS], U16, name="offsets", align_bytes=ROW_ALIGN)
         x_rows = xT.rearrange("(p l) w -> p l w", l=D)
         tables = []
         for level in range(D):
-            table = keep.tile([P, T], F32, name=f"table{level}")
+            table = keep.tile([P, T], F32, name=f"table{level}", align_bytes=ROW_ALIGN)
             if level < 2:
                 queue = nc.scalar if level == 1 else nc.sync
                 queue.dma_start(table[:], x_rows[:, level, :])
@@ -48,14 +49,14 @@ def tile_picked_grid_mlp_relu_sub_l_kernel(tc, xT, w1, w2, offs, out):
         w1_rows = w1.rearrange("(p j) i -> p j i", j=PACK)
         w1_raw = []
         for chunk in range(H // CHUNK):
-            raw = keep.tile([P, PACK, CHUNK], F32, name=f"w1_raw{chunk}", tag=f"w1_raw{chunk}", align_bytes=ALIGN)
+            raw = keep.tile([P, PACK, CHUNK], F32, name=f"w1_raw{chunk}", tag=f"w1_raw{chunk}", align_bytes=ROW_ALIGN)
             nc.sync.dma_start(raw[:], w1_rows[:, :, chunk * CHUNK : (chunk + 1) * CHUNK])
             w1_raw.append(raw)
         blocks = [slice(u * BLOCK, (u + 1) * BLOCK) for u in range(2)]
         w2_rows = w2.rearrange("(p j) n -> p j n", j=PACK)
         w2_raw = []
         for u, rows in enumerate(blocks):
-            raw = keep.tile([P, PACK, BLOCK], F32, name=f"w2_raw{u}", tag=f"w2_then_h{u}", align_bytes=ALIGN)
+            raw = keep.tile([P, PACK, BLOCK], F32, name=f"w2_raw{u}", tag=f"w2_then_h{u}", align_bytes=ROW_ALIGN)
             nc.sync.dma_start(raw[:], w2_rows[:, :, rows])
             w2_raw.append(raw)
 
@@ -143,7 +144,7 @@ def tile_picked_grid_mlp_relu_sub_l_kernel(tc, xT, w1, w2, offs, out):
             quantize_w1(t, slice(PART, P))
         for t in range(2, PACK):
             quantize_w1(t, slice(0, P))
-        x_codes.append(keep.tile([P, HALF], U32, name="x_codes1", tag="w1_raw3", align_bytes=ALIGN))
+        x_codes.append(keep.tile([P, HALF], U32, name="x_codes1", tag="w1_raw3", align_bytes=ROW_ALIGN))
         quantize(x_codes[1][:], x_scales[:, halves[1]], x_grouped[1][:])
 
         for half, v in enumerate(halves):
@@ -160,7 +161,7 @@ def tile_picked_grid_mlp_relu_sub_l_kernel(tc, xT, w1, w2, offs, out):
             quantize(w2_codes[:, rows], w2_scales[:, rows], w2_grouped[u][:])
 
         h_grouped = [
-            keep.tile([P, HALF, PACK], BF16, name=f"h_grouped{half}", tag=f"w2_then_h{half}", align_bytes=ALIGN)
+            keep.tile([P, HALF, PACK], BF16, name=f"h_grouped{half}", tag=f"w2_then_h{half}", align_bytes=ROW_ALIGN)
             for half in range(2)
         ]
         nc.scalar.activation(h_grouped[0][:], first[:].rearrange("p t v -> p v t"), RELU)
@@ -171,7 +172,7 @@ def tile_picked_grid_mlp_relu_sub_l_kernel(tc, xT, w1, w2, offs, out):
 
         out_view = out.rearrange("(u p) v -> p u v", u=2)
         for half, v in enumerate(halves):
-            result = keep.tile([P, 2, HALF], F32, name=f"result{half}")
+            result = keep.tile([P, 2, HALF], F32, name=f"result{half}", align_bytes=ROW_ALIGN)
             accs = [psum.tile([P, HALF], F32, name=f"acc{half}{u}") for u in range(2)]
             for u, rows in enumerate(blocks):
                 product(accs[u][:], w2_codes[:, rows], w2_scales[:, rows], h_codes[:, v], h_scales[:, v])

@@ -23,6 +23,7 @@ BLOCK = N // 2
 CHUNK = H // 4
 CHUNK_COLUMNS = CHUNK // PACK
 PART = 2 * CHUNK_COLUMNS
+W1_PIECES = (slice(0, 2 * CHUNK), slice(2 * CHUNK, 3 * CHUNK), slice(3 * CHUNK, H))
 LIST_COLUMNS = V // 16
 
 
@@ -48,9 +49,10 @@ def tile_picked_grid_mlp_relu_sub_l_kernel(tc, xT, w1, w2, offs, out):
                 nc.sync.dma_start(offsets[:], offs)
         w1_rows = w1.rearrange("(p j) i -> p j i", j=PACK)
         w1_raw = []
-        for chunk in range(H // CHUNK):
-            raw = keep.tile([P, PACK, CHUNK], F32, name=f"w1_raw{chunk}", tag=f"w1_raw{chunk}", align_bytes=ROW_ALIGN)
-            nc.sync.dma_start(raw[:], w1_rows[:, :, chunk * CHUNK : (chunk + 1) * CHUNK])
+        for piece, columns in enumerate(W1_PIECES):
+            width = columns.stop - columns.start
+            raw = keep.tile([P, PACK, width], F32, name=f"w1_raw{piece}", tag=f"w1_raw{piece}", align_bytes=ROW_ALIGN)
+            nc.sync.dma_start(raw[:], w1_rows[:, :, columns])
             w1_raw.append(raw)
         blocks = [slice(u * BLOCK, (u + 1) * BLOCK) for u in range(2)]
         w2_rows = w2.rearrange("(p j) n -> p j n", j=PACK)
@@ -66,7 +68,8 @@ def tile_picked_grid_mlp_relu_sub_l_kernel(tc, xT, w1, w2, offs, out):
             for half in range(2)
         ]
         x_scales = keep.tile([P, V], U8, name="x_scales", align_bytes=ALIGN)
-        w1_grouped = [keep.tile([P, 2, P, PACK], BF16, name=f"w1_grouped{pair}", align_bytes=ALIGN) for pair in range(2)]
+        low = [keep.tile([P, 2, PART, PACK], BF16, name=f"w1_low{part}", align_bytes=ALIGN) for part in range(2)]
+        high = keep.tile([P, 2, P, PACK], BF16, name="w1_high", align_bytes=ALIGN)
         w1_codes = [keep.tile([P, P], U32, name=f"w1_codes{t}", align_bytes=ALIGN) for t in range(PACK)]
         w1_scales = [keep.tile([P, P], U8, name=f"w1_scales{t}", align_bytes=ALIGN) for t in range(PACK)]
         w2_codes = keep.tile([P, N], U32, name="w2_codes", align_bytes=ALIGN)
@@ -83,14 +86,9 @@ def tile_picked_grid_mlp_relu_sub_l_kernel(tc, xT, w1, w2, offs, out):
                 in_=planes.rearrange("p j (c i) -> p c j i", i=4),
             )
 
-        def round_w1(copy, chunk, pair):
-            start = chunk * CHUNK_COLUMNS
-            dst = w1_grouped[pair][:, :, start : start + CHUNK_COLUMNS, :].rearrange("p t m j -> p m j t")
-            src = w1_raw[chunk][:].rearrange("p j (m t) -> p m j t", t=PACK)[:, :, :, 2 * pair : 2 * pair + 2]
-            copy(out=dst, in_=src)
-
-        def quantize_w1(t, m):
-            quantize(w1_codes[t][:, m], w1_scales[t][:, m], w1_grouped[t // 2][:, t % 2, m, :])
+        def round_w1(copy, grouped, piece, pair):
+            src = w1_raw[piece][:].rearrange("p j (m t) -> p m j t", t=PACK)[:, :, :, 2 * pair : 2 * pair + 2]
+            copy(out=grouped.rearrange("p t m j -> p m j t"), in_=src)
 
         def level_offsets(level, v0, v1):
             return offsets[:, level * LIST_COLUMNS + v0 // 16 : level * LIST_COLUMNS + v1 // 16]
@@ -121,30 +119,27 @@ def tile_picked_grid_mlp_relu_sub_l_kernel(tc, xT, w1, w2, offs, out):
         nc.scalar.activation(warm[:], zero[:].to_broadcast([P, 16]), RELU)
 
         nc.scalar.activation(x_picked[:, 1, :], tables[1].indirect(level_offsets(1, 0, V)), COPY)
-        nc.scalar.activation(x_picked[:, 3, HALF:V], tables[3].indirect(level_offsets(3, HALF, V)), COPY)
+        nc.scalar.activation(x_picked[:, 3, 0:HALF], tables[3].indirect(level_offsets(3, 0, HALF)), COPY)
         for level in (0, 2):
             gather(level, 0, V)
-        gather(3, 0, HALF)
+        gather(3, HALF, V)
 
-        round_w1(nc.scalar.copy, 0, 0)
-        round_w1(nc.scalar.copy, 0, 1)
-        round_w1(nc.scalar.copy, 1, 0)
-        round_w1(nc.scalar.copy, 2, 1)
-        round_w1(nc.scalar.copy, 3, 1)
-        for half in range(2):
-            interleave(nc.vector.tensor_copy, x_grouped[half][:], x_picked[:, :, halves[half]])
+        interleave(nc.scalar.copy, x_grouped[1][:], x_picked[:, :, halves[1]])
+        for piece, columns in enumerate(W1_PIECES):
+            round_w1(nc.scalar.copy, high[:, :, columns.start // PACK : columns.stop // PACK, :], piece, 1)
+        interleave(nc.vector.tensor_copy, x_grouped[0][:], x_picked[:, :, halves[0]])
+        round_w1(nc.vector.tensor_copy, low[0][:], 0, 0)
         x_codes = [keep.tile([P, HALF], U32, name="x_codes0", align_bytes=ALIGN)]
         quantize(x_codes[0][:], x_scales[:, halves[0]], x_grouped[0][:])
-        round_w1(nc.vector.tensor_copy, 1, 1)
-        round_w1(nc.vector.tensor_copy, 2, 0)
+        round_w1(nc.vector.tensor_copy, low[1][:, :, 0:CHUNK_COLUMNS, :], 1, 0)
         for t in range(2):
-            quantize_w1(t, slice(0, PART))
-        round_w1(nc.vector.tensor_copy, 3, 0)
+            quantize(w1_codes[t][:, 0:PART], w1_scales[t][:, 0:PART], low[0][:, t, :, :])
+        round_w1(nc.vector.tensor_copy, low[1][:, :, CHUNK_COLUMNS:PART, :], 2, 0)
         for t in range(2):
-            quantize_w1(t, slice(PART, P))
+            quantize(w1_codes[t][:, PART:P], w1_scales[t][:, PART:P], low[1][:, t, :, :])
         for t in range(2, PACK):
-            quantize_w1(t, slice(0, P))
-        x_codes.append(keep.tile([P, HALF], U32, name="x_codes1", tag="w1_raw3", align_bytes=ROW_ALIGN))
+            quantize(w1_codes[t][:], w1_scales[t][:], high[:, t - 2, :, :])
+        x_codes.append(keep.tile([P, HALF], U32, name="x_codes1", tag="w1_raw2", align_bytes=ROW_ALIGN))
         quantize(x_codes[1][:], x_scales[:, halves[1]], x_grouped[1][:])
 
         for half, v in enumerate(halves):

@@ -23,7 +23,7 @@ BLOCK = N // 2
 CHUNK = H // 4
 CHUNK_COLUMNS = CHUNK // PACK
 PART = 2 * CHUNK_COLUMNS
-W1_PIECES = (slice(0, 2 * CHUNK), slice(2 * CHUNK, 3 * CHUNK), slice(3 * CHUNK, H))
+W1_PIECES = tuple(slice(c * CHUNK, (c + 1) * CHUNK) for c in range(4))
 LIST_COLUMNS = V // 16
 
 
@@ -119,27 +119,30 @@ def tile_picked_grid_mlp_relu_sub_l_kernel(tc, xT, w1, w2, offs, out):
         nc.scalar.activation(warm[:], zero[:].to_broadcast([P, 16]), RELU)
 
         nc.scalar.activation(x_picked[:, 1, :], tables[1].indirect(level_offsets(1, 0, V)), COPY)
-        nc.scalar.activation(x_picked[:, 3, 0:HALF], tables[3].indirect(level_offsets(3, 0, HALF)), COPY)
+        nc.scalar.activation(x_picked[:, 3, HALF:V], tables[3].indirect(level_offsets(3, HALF, V)), COPY)
         for level in (0, 2):
             gather(level, 0, V)
-        gather(3, HALF, V)
+        gather(3, 0, HALF)
 
-        interleave(nc.scalar.copy, x_grouped[1][:], x_picked[:, :, halves[1]])
-        for piece, columns in enumerate(W1_PIECES):
-            round_w1(nc.scalar.copy, high[:, :, columns.start // PACK : columns.stop // PACK, :], piece, 1)
+        round_w1(nc.scalar.copy, low[0][:, :, 0:CHUNK_COLUMNS, :], 0, 0)
+        round_w1(nc.scalar.copy, high[:, :, 0:CHUNK_COLUMNS, :], 0, 1)
+        round_w1(nc.scalar.copy, low[0][:, :, CHUNK_COLUMNS:PART, :], 1, 0)
         interleave(nc.vector.tensor_copy, x_grouped[0][:], x_picked[:, :, halves[0]])
-        round_w1(nc.vector.tensor_copy, low[0][:], 0, 0)
+        interleave(nc.vector.tensor_copy, x_grouped[1][:], x_picked[:, :, halves[1]])
         x_codes = [keep.tile([P, HALF], U32, name="x_codes0", align_bytes=ALIGN)]
         quantize(x_codes[0][:], x_scales[:, halves[0]], x_grouped[0][:])
-        round_w1(nc.vector.tensor_copy, low[1][:, :, 0:CHUNK_COLUMNS, :], 1, 0)
+        round_w1(nc.vector.tensor_copy, high[:, :, CHUNK_COLUMNS:PART, :], 1, 1)
+        round_w1(nc.scalar.copy, high[:, :, PART : PART + CHUNK_COLUMNS, :], 2, 1)
+        round_w1(nc.scalar.copy, high[:, :, PART + CHUNK_COLUMNS : P, :], 3, 1)
+        round_w1(nc.vector.tensor_copy, low[1][:, :, 0:CHUNK_COLUMNS, :], 2, 0)
         for t in range(2):
             quantize(w1_codes[t][:, 0:PART], w1_scales[t][:, 0:PART], low[0][:, t, :, :])
-        round_w1(nc.vector.tensor_copy, low[1][:, :, CHUNK_COLUMNS:PART, :], 2, 0)
+        round_w1(nc.vector.tensor_copy, low[1][:, :, CHUNK_COLUMNS:PART, :], 3, 0)
         for t in range(2):
             quantize(w1_codes[t][:, PART:P], w1_scales[t][:, PART:P], low[1][:, t, :, :])
         for t in range(2, PACK):
             quantize(w1_codes[t][:], w1_scales[t][:], high[:, t - 2, :, :])
-        x_codes.append(keep.tile([P, HALF], U32, name="x_codes1", tag="w1_raw2", align_bytes=ROW_ALIGN))
+        x_codes.append(keep.tile([P, HALF], U32, name="x_codes1", tag="w1_raw3", align_bytes=ROW_ALIGN))
         quantize(x_codes[1][:], x_scales[:, halves[1]], x_grouped[1][:])
 
         for half, v in enumerate(halves):

@@ -24,6 +24,7 @@ CHUNK = H // 4
 CHUNK_COLUMNS = CHUNK // PACK
 PART = 2 * CHUNK_COLUMNS
 W1_PIECES = tuple(slice(c * CHUNK, (c + 1) * CHUNK) for c in range(4))
+WARM_ROWS, WARM_PASSES = 32, 4
 LIST_COLUMNS = V // 16
 
 
@@ -137,6 +138,9 @@ def tile_picked_grid_mlp_relu_sub_l_kernel(tc, xT, w1, w2, offs, out):
         round_w1(nc.vector.tensor_copy, low[1][:, :, 0:CHUNK_COLUMNS, :], 2, 0)
         for t in range(2):
             quantize(w1_codes[t][:, 0:PART], w1_scales[t][:, 0:PART], low[0][:, t, :, :])
+        idle = psum.tile([WARM_ROWS, WARM_PASSES, HALF], F32, name="idle")
+        for i in range(WARM_PASSES):
+            product(idle[:, i, :], w1_codes[1][:, 0:WARM_ROWS], w1_scales[1][:, 0:WARM_ROWS], x_codes[0][:], x_scales[:, halves[0]])
         round_w1(nc.vector.tensor_copy, low[1][:, :, CHUNK_COLUMNS:PART, :], 3, 0)
         for t in range(2):
             quantize(w1_codes[t][:, PART:P], w1_scales[t][:, PART:P], low[1][:, t, :, :])

from contextlib import ExitStack

import concourse.mybir as mybir

K, T, D, V, H, N = 512, 512, 4, 256, 512, 256
P = 128
FLOPS = 2 * K * H * V + 2 * H * N * V

F32 = mybir.dt.float32
BF16 = mybir.dt.bfloat16
U32 = mybir.dt.uint32
U16 = mybir.dt.uint16
U8 = mybir.dt.uint8
FP8X4 = mybir.dt.float8_e4m3fn_x4
RELU = mybir.ActivationFunctionType.Relu
COPY = mybir.ActivationFunctionType.Copy

PACK = 4
ALIGN = 64
ROW_ALIGN = 256
HALF = V // 2
BLOCK = N // 2
CHUNK = H // 4
CHUNK_COLUMNS = CHUNK // PACK
PART = 2 * CHUNK_COLUMNS
W1_PIECES = tuple(slice(c * CHUNK, (c + 1) * CHUNK) for c in range(4))
WARM_ROWS, WARM_PASSES = 32, 4
LIST_COLUMNS = V // 16


def tile_picked_grid_mlp_relu_sub_l_kernel(tc, xT, w1, w2, offs, out):
    nc = tc.nc
    with ExitStack() as ctx:
        keep = ctx.enter_context(tc.tile_pool(name="keep", bufs=1))
        psum = ctx.enter_context(tc.psum_pool(name="psum", bufs=1))

        offsets = keep.tile([P, D * LIST_COLUMNS], U16, name="offsets", align_bytes=ROW_ALIGN)
        x_rows = xT.rearrange("(p l) w -> p l w", l=D)
        tables = []
        for level in range(D):
            table = keep.tile([P, T], F32, name=f"table{level}", align_bytes=ROW_ALIGN)
            if level < 2:
                queue = nc.scalar if level == 1 else nc.sync
                queue.dma_start(table[:], x_rows[:, level, :])
            else:
                nc.sync.dma_start(table[:, 0 : T // 2], x_rows[:, level, 0 : T // 2])
                nc.scalar.dma_start(table[:, T // 2 : T], x_rows[:, level, T // 2 : T])
            tables.append(table[:])
            if level == 0:
                nc.sync.dma_start(offsets[:], offs)
        w1_rows = w1.rearrange("(p j) i -> p j i", j=PACK)
        w1_raw = []
        for piece, columns in enumerate(W1_PIECES):
            width = columns.stop - columns.start
            raw = keep.tile([P, PACK, width], F32, name=f"w1_raw{piece}", tag=f"w1_raw{piece}", align_bytes=ROW_ALIGN)
            nc.sync.dma_start(raw[:], w1_rows[:, :, columns])
            w1_raw.append(raw)
        blocks = [slice(u * BLOCK, (u + 1) * BLOCK) for u in range(2)]
        w2_rows = w2.rearrange("(p j) n -> p j n", j=PACK)
        w2_raw = []
        for u, rows in enumerate(blocks):
            raw = keep.tile([P, PACK, BLOCK], F32, name=f"w2_raw{u}", tag=f"w2_then_h{u}", align_bytes=ROW_ALIGN)
            nc.sync.dma_start(raw[:], w2_rows[:, :, rows])
            w2_raw.append(raw)

        x_picked = keep.tile([P, D, V], BF16, name="x_picked", align_bytes=ALIGN)
        x_grouped = [
            keep.tile([P, HALF, PACK], BF16, name=f"x_grouped{half}", tag=f"x_then_w2{half}", align_bytes=ALIGN)
            for half in range(2)
        ]
        x_scales = keep.tile([P, V], U8, name="x_scales", align_bytes=ALIGN)
        low = [keep.tile([P, 2, PART, PACK], BF16, name=f"w1_low{part}", align_bytes=ALIGN) for part in range(2)]
        high = keep.tile([P, 2, P, PACK], BF16, name="w1_high", align_bytes=ALIGN)
        w1_codes = [keep.tile([P, P], U32, name=f"w1_codes{t}", align_bytes=ALIGN) for t in range(PACK)]
        w1_scales = [keep.tile([P, P], U8, name=f"w1_scales{t}", align_bytes=ALIGN) for t in range(PACK)]
        w2_codes = keep.tile([P, N], U32, name="w2_codes", align_bytes=ALIGN)
        w2_scales = keep.tile([P, N], U8, name="w2_scales", align_bytes=ALIGN)
        h_codes = keep.tile([P, V], U32, name="h_codes", align_bytes=ALIGN)
        h_scales = keep.tile([P, V], U8, name="h_scales", align_bytes=ALIGN)

        def quantize(codes, scales, grouped):
            nc.vector.quantize_mx(out=codes.bitcast(FP8X4), scales=scales, in_=grouped.rearrange("p c j -> p (c j)"))

        def interleave(copy, grouped, planes):
            copy(
                out=grouped.rearrange("p (c i) j -> p c j i", i=4),
                in_=planes.rearrange("p j (c i) -> p c j i", i=4),
            )

        def round_w1(copy, grouped, piece, pair):
            src = w1_raw[piece][:].rearrange("p j (m t) -> p m j t", t=PACK)[:, :, :, 2 * pair : 2 * pair + 2]
            copy(out=grouped.rearrange("p t m j -> p m j t"), in_=src)

        def level_offsets(level, v0, v1):
            return offsets[:, level * LIST_COLUMNS + v0 // 16 : level * LIST_COLUMNS + v1 // 16]

        def gather(level, v0, v1):
            picked = x_picked[:, level, v0:v1]
            nc.vector.tensor_copy(picked, tables[level].indirect(level_offsets(level, v0, v1)))

        def product(acc, codes, scales, moving, moving_scales):
            nc.tensor.matmul_mx(
                out=acc,
                lhsT=codes.bitcast(FP8X4),
                lhsT_scale=scales,
                rhs=moving.bitcast(FP8X4),
                rhs_scale=moving_scales,
                start=True,
                stop=True,
            )

        halves = [slice(half * HALF, (half + 1) * HALF) for half in range(2)]
        first = psum.tile([P, PACK, HALF], F32, name="hidden0")
        second = [psum.tile([P, 2, HALF], F32, name=f"hidden1{pair}") for pair in range(2)]
        hidden = [[first[:, t, :] for t in range(PACK)], [second[t // 2][:, t % 2, :] for t in range(PACK)]]

        zero = keep.tile([P, 1], F32, name="zero")
        nc.vector.memset(zero[:], 0.0)
        warm = keep.tile([P, 16], F32, name="warm")
        nc.scalar.activation(warm[:], zero[:].to_broadcast([P, 16]), RELU)

        nc.scalar.activation(x_picked[:, 1, :], tables[1].indirect(level_offsets(1, 0, V)), COPY)
        nc.scalar.activation(x_picked[:, 3, HALF:V], tables[3].indirect(level_offsets(3, HALF, V)), COPY)
        for level in (0, 2):
            gather(level, 0, V)
        gather(3, 0, HALF)

        round_w1(nc.scalar.copy, low[0][:, :, 0:CHUNK_COLUMNS, :], 0, 0)
        round_w1(nc.scalar.copy, high[:, :, 0:CHUNK_COLUMNS, :], 0, 1)
        round_w1(nc.scalar.copy, low[0][:, :, CHUNK_COLUMNS:PART, :], 1, 0)
        interleave(nc.vector.tensor_copy, x_grouped[0][:], x_picked[:, :, halves[0]])
        interleave(nc.vector.tensor_copy, x_grouped[1][:], x_picked[:, :, halves[1]])
        x_codes = [keep.tile([P, HALF], U32, name="x_codes0", align_bytes=ALIGN)]
        quantize(x_codes[0][:], x_scales[:, halves[0]], x_grouped[0][:])
        round_w1(nc.vector.tensor_copy, high[:, :, CHUNK_COLUMNS:PART, :], 1, 1)
        round_w1(nc.scalar.copy, high[:, :, PART : PART + CHUNK_COLUMNS, :], 2, 1)
        round_w1(nc.scalar.copy, high[:, :, PART + CHUNK_COLUMNS : P, :], 3, 1)
        round_w1(nc.vector.tensor_copy, low[1][:, :, 0:CHUNK_COLUMNS, :], 2, 0)
        for t in range(2):
            quantize(w1_codes[t][:, 0:PART], w1_scales[t][:, 0:PART], low[0][:, t, :, :])
        idle = psum.tile([WARM_ROWS, WARM_PASSES, HALF], F32, name="idle")
        for i in range(WARM_PASSES):
            product(idle[:, i, :], w1_codes[1][:, 0:WARM_ROWS], w1_scales[1][:, 0:WARM_ROWS], x_codes[0][:], x_scales[:, halves[0]])
        round_w1(nc.vector.tensor_copy, low[1][:, :, CHUNK_COLUMNS:PART, :], 3, 0)
        for t in range(2):
            quantize(w1_codes[t][:, PART:P], w1_scales[t][:, PART:P], low[1][:, t, :, :])
        for t in range(2, PACK):
            quantize(w1_codes[t][:], w1_scales[t][:], high[:, t - 2, :, :])
        x_codes.append(keep.tile([P, HALF], U32, name="x_codes1", tag="w1_raw3", align_bytes=ROW_ALIGN))
        quantize(x_codes[1][:], x_scales[:, halves[1]], x_grouped[1][:])

        for half, v in enumerate(halves):
            for t in range(PACK):
                product(hidden[half][t], w1_codes[t][:], w1_scales[t][:], x_codes[half][:], x_scales[:, v])

        w2_grouped = [
            keep.tile([P, BLOCK, PACK], BF16, name="w2_grouped0", align_bytes=ALIGN),
            keep.tile([P, BLOCK, PACK], BF16, name="w2_grouped1", tag="x_then_w21", align_bytes=ALIGN),
        ]
        interleave(nc.scalar.copy, w2_grouped[0][:], w2_raw[0][:])
        interleave(nc.vector.tensor_copy, w2_grouped[1][:], w2_raw[1][:])
        for u, rows in enumerate(blocks):
            quantize(w2_codes[:, rows], w2_scales[:, rows], w2_grouped[u][:])

        h_grouped = [
            keep.tile([P, HALF, PACK], BF16, name=f"h_grouped{half}", tag=f"w2_then_h{half}", align_bytes=ROW_ALIGN)
            for half in range(2)
        ]
        nc.scalar.activation(h_grouped[0][:], first[:].rearrange("p t v -> p v t"), RELU)
        nc.scalar.activation(h_grouped[1][:, :, 2:4], second[1][:].rearrange("p t v -> p v t"), RELU)
        nc.vector.tensor_scalar_max(h_grouped[1][:, :, 0:2], second[0][:].rearrange("p t v -> p v t"), zero[:])
        for half, v in enumerate(halves):
            quantize(h_codes[:, v], h_scales[:, v], h_grouped[half][:])

        out_view = out.rearrange("(u p) v -> p u v", u=2)
        for half, v in enumerate(halves):
            result = keep.tile([P, 2, HALF], F32, name=f"result{half}", align_bytes=ROW_ALIGN)
            accs = [psum.tile([P, HALF], F32, name=f"acc{half}{u}") for u in range(2)]
            for u, rows in enumerate(blocks):
                product(accs[u][:], w2_codes[:, rows], w2_scales[:, rows], h_codes[:, v], h_scales[:, v])
            nc.scalar.copy(result[:, 0, :], accs[0][:])
            nc.vector.tensor_copy(result[:, 1, :], accs[1][:])
            if half == 0:
                nc.sync.dma_start(out_view[:, :, v], result[:])
            else:
                nc.scalar.dma_start(out_view[:, 0, v], result[:, 0, :])
                nc.sync.dma_start(out_view[:, 1, v], result[:, 1, :])
